import numpy as np
import ml_dtypes


def mxq(x, axis, fmt="e4m3"):
    dtype, down = {"e4m3": (ml_dtypes.float8_e4m3fn, 7), "e5m2": (ml_dtypes.float8_e5m2, 14)}[fmt]
    v = np.moveaxis(np.asarray(x, np.float32).astype(ml_dtypes.bfloat16).astype(np.float64), axis, -1)
    blocks = v.reshape(v.shape[:-1] + (-1, 32))
    amax = np.abs(blocks).max(-1, keepdims=True)
    byte = np.maximum(np.where(amax > 0, np.frexp(amax)[1] - 1 + 127, 0) - down, 1)
    scale = np.exp2(byte - 127.0)
    codes = (blocks / scale).astype(np.float32).astype(dtype).astype(np.float64)
    return np.moveaxis((codes * scale).reshape(v.shape), -1, axis)


WIDE = False


def mx_kscale(k):
    if not WIDE:
        return np.ones(k)
    levels = np.array([10, -10, 5, -5, 0])
    if k % 512:
        return np.exp2(np.random.permutation(np.resize(levels, k // 32))).repeat(32)
    a = np.empty((k // 512, 16))
    for p in range(k // 512):
        a[p, :8] = np.random.permutation(np.resize(levels, 8))
        for g in range(8):
            far = levels[np.abs(levels - a[p, g]) >= 10]
            a[p, g + 8] = far[np.random.randint(len(far))]
    return np.exp2(a.ravel()).repeat(32)


def f64(x):
    return np.asarray(x).astype(np.float64)


def striped(idx):
    return np.tile(idx.reshape(-1, 16).T, (8, 1)).astype(np.uint16)


def unstriped(offs):
    return offs[:16].T.reshape(-1).astype(np.int64)


E2M1 = np.array([0.0, 0.5, 1.0, 1.5, 2.0, 3.0, 4.0, 6.0, -0.0, -0.5, -1.0, -1.5, -2.0, -3.0, -4.0, -6.0])


def pack_weight(w, fmt):
    k, n = w.shape
    w = f64(np.asarray(w, np.float32).astype(ml_dtypes.bfloat16)).reshape(k // 32, 32, n)
    amax = np.abs(w).max(1)
    if fmt == "e4m3":
        byte = np.frexp(amax)[1] - 1 + 127 - 7
    else:
        mant, ex = np.frexp(amax / 6.0)
        byte = np.where(mant > 0.5, ex, ex - 1) + 127
    byte = np.clip(np.where(amax > 0, byte, 1), 1, 254)
    scaled = (w * np.exp2(127.0 - byte)[:, None, :]).reshape(k, n).astype(np.float32)
    by_word = np.ascontiguousarray(scaled.reshape(k // 512, 128, 4, n).transpose(0, 1, 3, 2))
    if fmt == "e4m3":
        words = by_word.astype(ml_dtypes.float8_e4m3fn).view(np.uint8)
    else:
        c = by_word.astype(ml_dtypes.float4_e2m1fn).view(np.uint8) & 0xF
        words = (c[..., 0::2] | (c[..., 1::2] << 4)).reshape(k // 512, 128, 2 * n)
    return np.ascontiguousarray(words), np.ascontiguousarray(byte.astype(np.uint8).reshape(k // 512, 16, n))


def unpack_weight(words, scales, fmt):
    g, _, n = scales.shape
    words = np.ascontiguousarray(words).reshape(g, 128, n, -1)
    if fmt == "e4m3":
        vals = words.view(ml_dtypes.float8_e4m3fn).astype(np.float64)
    else:
        nib = np.empty((g, 128, n, 4), np.uint8)
        nib[..., 0::2] = words & 0xF
        nib[..., 1::2] = words >> 4
        vals = E2M1[nib]
    vals = vals * np.repeat(np.exp2(scales.astype(np.float64) - 127.0), 8, axis=1)[..., None]
    return vals.transpose(0, 1, 3, 2).reshape(g * 512, n)


def gelu(v):
    return 0.5 * v * (1.0 + np.tanh(np.sqrt(2.0 / np.pi) * (v + 0.044715 * v**3)))


K, K2, T, TB, S, H, T2, N = 1024, 512, 2048, 1024, 512, 1024, 1024, 512


def setup_inputs():
    n = np.random.standard_normal
    s = mx_kscale(K)[:, None]
    s2 = mx_kscale(K2)[:, None]
    u = mx_kscale(H)[:, None]
    tab_words, tab_scales = pack_weight(n((K, T)) * s, "e4m3")
    tab2_words, tab2_scales = pack_weight(n((K2, TB)) * s2, "e4m3")
    w2_words, w2_scales = pack_weight(n((K, H)) / np.sqrt(K) / s, "e2m1")
    w4_words, w4_scales = pack_weight(n((K2, H)) / np.sqrt(K2) / s2, "e4m3")
    return {
        "tab_words": tab_words, "tab_scales": tab_scales,
        "tab2_words": tab2_words, "tab2_scales": tab2_scales,
        "offs": striped(np.random.permutation(T)[:S]),
        "offs2": striped(np.random.permutation(TB)[:S]),
        "offs3": striped(np.random.permutation(T2)[:S]),
        "offs4": striped(np.random.permutation(T2)[:S]),
        "w1": (n((K, H)) / np.sqrt(K) / s).astype(np.float32),
        "w2_words": w2_words, "w2_scales": w2_scales,
        "w3": (n((K2, H)) / np.sqrt(K2) / s2).astype(np.float32),
        "w4_words": w4_words, "w4_scales": w4_scales,
        "wg1": np.exp(0.3 * n((128, S))).astype(np.float32),
        "wg2": np.exp(0.3 * n((128, S))).astype(np.float32),
        "oldmap": (0.7 * n((H, T2)) * u).astype(np.float32),
        "w5": (n((H, N)) / np.sqrt(H) / u).astype(np.float32),
    }


def reference(tab_words, tab_scales, tab2_words, tab2_scales, offs, offs2, offs3, offs4, w1, w2_words, w2_scales, w3, w4_words, w4_scales, wg1, wg2, oldmap, w5):
    v = unpack_weight(tab_words, tab_scales, "e4m3")[:, unstriped(offs)]
    v2 = unpack_weight(tab2_words, tab2_scales, "e4m3")[:, unstriped(offs2)]
    a1 = mxq(f64(w1), 0, "e4m3").T @ v
    a2 = unpack_weight(w2_words, w2_scales, "e2m1").T @ v
    h1 = np.maximum(a1, a2)
    b1 = mxq(f64(w3), 0, "e4m3").T @ v2
    b2 = unpack_weight(w4_words, w4_scales, "e4m3").T @ v2
    h2 = b1 * b2
    pa = np.zeros((H, T2))
    pa[:, unstriped(offs3)] = np.tile(f64(wg1), (H // 128, 1)) * h1
    pb = np.zeros((H, T2))
    pb[:, unstriped(offs4)] = np.tile(f64(wg2), (H // 128, 1)) * h2
    z = f64(oldmap) * (1.0 + np.abs(pa + pb))
    y = mxq(f64(w5), 0, "e4m3").T @ mxq(z, 0, "e4m3")
    return np.tanh(y)

@@ -1,0 +1,332 @@
+from contextlib import ExitStack
+
+import concourse.mybir as mybir
+from concourse.masks import make_identity
+
+K, K2, T, TB, S, H, T2, N = 1024, 512, 2048, 1024, 512, 1024, 1024, 512
+FLOPS = 2 * S * H * (2 * K + 2 * K2) + 2 * H * N * T2
+
+F32 = mybir.dt.float32
+BF16 = mybir.dt.bfloat16
+I32 = mybir.dt.int32
+U32 = mybir.dt.uint32
+U16 = mybir.dt.uint16
+U8 = mybir.dt.uint8
+FP8X4 = mybir.dt.float8_e4m3fn_x4
+FP4X4 = mybir.dt.float4_e2m1fn_x4
+ALU = mybir.AluOpType
+ACT = mybir.ActivationFunctionType
+
+P = 128
+PACK = 4
+K_PASS = P * PACK
+BANK = 512
+CHUNK = 256
+SLICES = H // P
+PAGES_A = 2
+PAGES_B = 4
+W3_WIDTHS = (128, 128, 256, 256, 256)
+W4_HEAD = 256
+
+
+def tile_list_street_change_scores_kernel(
+    tc, tab_words, tab_scales, tab2_words, tab2_scales, offs, offs2, offs3, offs4,
+    w1, w2_words, w2_scales, w3, w4_words, w4_scales, wg1, wg2, oldmap, w5, out,
+):
+    nc = tc.nc
+    with ExitStack() as ctx:
+        keep = ctx.enter_context(tc.tile_pool(name="keep", bufs=1))
+        ring = ctx.enter_context(tc.tile_pool(name="ring", bufs=2))
+        psum = ctx.enter_context(tc.psum_pool(name="psum", bufs=2))
+
+        def held(name, shape, dtype, tag=None):
+            return keep.tile(shape, dtype, name=name, tag=tag or name, align_bytes=64)
+
+        def load_list(name, source):
+            tile = held(name, [P, S // 16], U16)
+            nc.sync.dma_start(tile[:], source)
+            return tile
+
+        def load_words(name, source, dtype):
+            width = source.shape[1] if dtype == U8 else source.shape[1] // 4
+            tile = held(name, [P, width], dtype)
+            nc.sync.dma_start(tile[:].bitcast(I32), source.bitcast(I32))
+            return tile
+
+        def cleared_plane(name, source):
+            tile = held(name, [P, source.shape[0] * source.shape[2]], U8)
+            nc.gpsimd.memset(tile[:].bitcast(I32), 0)
+            return tile
+
+        def load_plane(tile, source):
+            passes = source.shape[0]
+            for q in range(4):
+                nc.sync.dma_start(
+                    tile[32 * q : 32 * q + 4, :].bitcast(I32).rearrange("r (a t) -> r a t", a=passes),
+                    source[:, 4 * q : 4 * q + 4, :].bitcast(I32).rearrange("a r t -> r a t"),
+                )
+
+        def load_rows(source, a, c0, tag="raw", bufs=11, width=CHUNK):
+            raw = ring.tile([P, PACK, width], F32, name="raw", tag=tag, bufs=bufs, align_bytes=64)
+            rows = source[a * K_PASS : (a + 1) * K_PASS, c0 : c0 + width]
+            nc.sync.dma_start(raw[:], rows.rearrange("(p t) c -> p t c", t=PACK))
+            return raw
+
+        def weave(copy, dst, src):
+            copy(dst.rearrange("p (c i t) -> p c t i", i=2, t=PACK), src.rearrange("p t (c i) -> p c t i", i=2))
+
+        def quantised(name, raws, copy, stage_tag=None, codes_tag=None):
+            each = raws[0].shape[2]
+            width = len(raws) * each
+            if stage_tag:
+                stage = held(stage_tag, [P, PACK * width], BF16)
+            else:
+                stage = ring.tile([P, PACK * width], BF16, name="stage", tag="woven", bufs=6, align_bytes=64)
+            for a, raw in enumerate(raws):
+                weave(copy, stage[:, a * PACK * each : (a + 1) * PACK * each], raw[:])
+            codes = held(name + "_codes", [P, width], U32, codes_tag)
+            scales = held(name + "_scales", [P, width], U8)
+            nc.vector.quantize_mx(out=codes[:].bitcast(FP8X4), scales=scales[:], in_=stage[:])
+            return codes, scales
+
+        def gathered(name, window, offsets, dtype):
+            tile = held(name, [P, S], dtype)
+            nc.vector.tensor_copy(tile[:], window.indirect(offsets[:]))
+            return tile
+
+        tab2_plane = cleared_plane("tab2_plane", tab2_scales)
+        w4_plane = cleared_plane("w4_plane", w4_scales)
+        pages_b = [held("page_b%d" % i, [P, T2], F32) for i in range(PAGES_B)]
+        pages_a = [held("page_a%d" % i, [P, T2], F32) for i in range(PAGES_A)]
+        tab_plane = cleared_plane("tab_plane", tab_scales)
+        nc.gpsimd.memset(pages_b[0][:], 0.0)
+        w2_plane = cleared_plane("w2_plane", w2_scales)
+        ident = held("ident", [P, P], F32)
+        make_identity(nc, ident[:])
+        for page in pages_b[1:] + pages_a:
+            nc.gpsimd.memset(page[:], 0.0)
+
+        flat = "p t i -> p (t i)"
+        w3_starts = [sum(W3_WIDTHS[:j]) for j in range(len(W3_WIDTHS))]
+        w4_flat = w4_words[0].rearrange(flat)
+        list2 = load_list("list2", offs2)
+        load_plane(tab2_plane, tab2_scales)
+        tab2_sb = load_words("tab2_sb", tab2_words[0].rearrange(flat), U32)
+        w3_raw = [load_rows(w3, 0, 0, width=W3_WIDTHS[0])]
+        w4_head = load_words("w4_head", w4_flat[:, : 4 * W4_HEAD], U32)
+        load_plane(w4_plane, w4_scales)
+        w3_raw.append(load_rows(w3, 0, w3_starts[1], width=W3_WIDTHS[1]))
+        list4 = load_list("list4", offs4)
+        wg2_sb = held("wg2_sb", [P, S], F32)
+        nc.sync.dma_start(wg2_sb[:], wg2)
+        w3_raw.append(load_rows(w3, 0, w3_starts[2], width=W3_WIDTHS[2]))
+        w4_rest = load_words("w4_rest", w4_flat[:, 4 * W4_HEAD :], U32)
+        list1 = load_list("list1", offs)
+        load_plane(tab_plane, tab_scales)
+        for j in (3, 4):
+            w3_raw.append(load_rows(w3, 0, w3_starts[j], width=W3_WIDTHS[j]))
+        w1_raw = [[load_rows(w1, a, j * CHUNK) for a in range(2)] for j in range(H // CHUNK - 1)]
+        w1_raw.append([load_rows(w1, 0, H - CHUNK), load_rows(w1, 1, H - CHUNK, "raw_last", 1)])
+        load_plane(w2_plane, w2_scales)
+        w2_sb = [load_words("w2_sb%d" % a, w2_words[a], U8) for a in range(2)]
+        list3 = load_list("list3", offs3)
+        wg1_sb = held("wg1_sb", [P, S], F32)
+        nc.sync.dma_start(wg1_sb[:], wg1)
+        tab_sb = [load_words("tab_sb%d" % a, tab_words[a].rearrange(flat), U32) for a in range(2)]
+
+        v2_scales = gathered("v2_scales", tab2_plane[:], list2, U8)
+        v2_words = gathered("v2_words", tab2_sb[:], list2, U32)
+
+        w3_q, w1_q, w5_q = {}, {}, {}
+        v_words, v_scales = [], []
+        old_raw, old_woven, sums, absum, features = {}, {}, {}, {}, {}
+        z_q = {}
+
+        def mx(bank, lhs, lhs_scale, rhs, rhs_scale, start, stop):
+            nc.tensor.matmul_mx(out=bank, lhsT=lhs, lhsT_scale=lhs_scale, rhs=rhs.bitcast(FP8X4),
+                                rhs_scale=rhs_scale, start=start, stop=stop)
+
+        def product_bank(tag):
+            return psum.tile([P, BANK], F32, name=tag, tag=tag, bufs=1 if tag == "first" else 3)
+
+        def staged(first, second, op, late=False):
+            if late:
+                copied = ring.tile([P, S], F32, name="copied", tag="raw_last", bufs=1, align_bytes=64)
+            else:
+                copied = ring.tile([P, S], F32, name="copied", tag="copied", bufs=3)
+            nc.scalar.copy(copied[:], first[:])
+            return copied, second, op
+
+        def combine(copied, second, op, tag=None):
+            if tag:
+                feature = held("feature_held", [P, S], F32, tag)
+            else:
+                feature = ring.tile([P, S], F32, name="feature", tag="feature", bufs=3)
+            nc.vector.tensor_tensor(feature[:], second[:], copied[:], op)
+            return feature
+
+        def quality(c):
+            cols = slice(c * P, (c + 1) * P)
+            j = max(i for i, start in enumerate(w3_starts) if start <= c * P)
+            codes, scales = w3_q[j]
+            local = slice(c * P - w3_starts[j], (c + 1) * P - w3_starts[j])
+            w4_cols = w4_head[:, cols] if c * P < W4_HEAD else w4_rest[:, c * P - W4_HEAD : (c + 1) * P - W4_HEAD]
+            b2, b1 = product_bank("first"), product_bank("second")
+            mx(b2[:], w4_cols.bitcast(FP8X4), w4_plane[:, cols], v2_words[:], v2_scales[:], True, True)
+            mx(b1[:], codes[:, local].bitcast(FP8X4), scales[:, local], v2_words[:], v2_scales[:], True, True)
+            return staged(b2, b1, ALU.mult, c == 4)
+
+        def facade(c):
+            j = c // 2
+            codes, scales = w1_q[j]
+            a2, a1 = product_bank("first"), product_bank("second")
+            for a in range(2):
+                mx(a2[:], w2_sb[a][:, 2 * c * P : 2 * (c + 1) * P].bitcast(FP4X4),
+                   w2_plane[:, a * H + c * P : a * H + (c + 1) * P], v_words[a][:], v_scales[a][:], a == 0, a == 1)
+            for a in range(2):
+                local = slice(a * CHUNK + (c % 2) * P, a * CHUNK + (c % 2 + 1) * P)
+                mx(a1[:], codes[:, local].bitcast(FP8X4), scales[:, local], v_words[a][:], v_scales[a][:], a == 0, a == 1)
+            return staged(a2, a1, ALU.max)
+
+        def turn(bank, page, half, start, stop):
+            for i in range(4):
+                m0 = (4 * half + i) * P
+                nc.tensor.matmul(bank[:, i * P : (i + 1) * P], page[:, m0 : m0 + P], ident[:],
+                                 start=start and i == 0, stop=stop and i == 3, is_transpose=True)
+
+        def open_sum(c):
+            sums[c] = [psum.tile([P, BANK], F32, name="sum", tag="sum", bufs=2) for half in range(2)]
+            for half in range(2):
+                turn(sums[c][half], pages_b[c % PAGES_B], half, True, False)
+
+        def close_sum(c):
+            b, quarter = divmod(c, 4)
+            for half in range(2):
+                if quarter == 0 and (b, half) == (1, 1):
+                    absum[b, half] = held("absum_last", [P, 4, PACK, P], F32, "tab_sb0")
+                elif quarter == 0:
+                    absum[b, half] = ring.tile([P, 4, PACK, P], F32, name="absum", tag="absum", bufs=3)
+                turn(sums[c][half], pages_a[c % PAGES_A], half, False, True)
+                nc.scalar.activation(
+                    absum[b, half][:, :, :, 32 * quarter : 32 * quarter + 32],
+                    sums[c][half][:].rearrange("m (i q t) -> m i t q", i=4, t=PACK), ACT.Abs)
+
+        def load_old(b):
+            old_raw[b] = ring.tile([P, PACK, T2], F32, name="old_raw", tag="old_raw", bufs=1)
+            nc.sync.dma_start(old_raw[b][:], oldmap[b * K_PASS : (b + 1) * K_PASS, :].rearrange("(p t) m -> p t m", t=PACK))
+
+        def weave_old(b, q):
+            old_woven[b, q] = ring.tile([P, PACK * CHUNK], F32, name="old_woven", tag="raw" if b else "woven",
+                                        bufs=11 if b else 6, align_bytes=64)
+            weave(nc.scalar.copy, old_woven[b, q][:], old_raw[b][:, :, q * CHUNK : (q + 1) * CHUNK])
+
+        def strengthened(b, m0, width, tag=None):
+            if tag:
+                z = held("z_on_" + tag, [P, PACK * CHUNK], BF16, tag)
+            else:
+                z = ring.tile([P, PACK * CHUNK], BF16, name="z", tag="z", bufs=3, align_bytes=64)
+            for i in range(width // P):
+                mc = m0 // P + i
+                back = psum.tile([P, PACK, P], F32, name="back", tag="sum" if b == 1 and mc % 4 >= 2 else "back", bufs=2)
+                for t in range(PACK):
+                    nc.tensor.transpose(back[:, t, :], absum[b, mc // 4][:, mc % 4, t, :], ident[:])
+                part = slice((mc % 2) * BANK, (mc % 2 + 1) * BANK)
+                nc.vector.scalar_tensor_tensor(
+                    z[:, i * BANK : (i + 1) * BANK].rearrange("p (m t) -> p m t", t=PACK),
+                    back[:].rearrange("p t m -> p m t"), 1.0,
+                    old_woven[b, mc // 2][:, part].rearrange("p (m t) -> p m t", t=PACK), ALU.add, ALU.mult)
+            codes = held("z_codes%d_%d" % (b, m0), [P, width], U32)
+            scales = held("z_scales%d_%d" % (b, m0), [P, width], U8)
+            nc.vector.quantize_mx(out=codes[:].bitcast(FP8X4), scales=scales[:], in_=z[:, : PACK * width])
+            for i in range(width // P):
+                z_q[b, m0 // P + i] = (codes[:, i * P : (i + 1) * P], scales[:, i * P : (i + 1) * P])
+
+        results = {}
+
+        def scores(mc):
+            bank = product_bank("first" if mc % 4 == 3 else "second")
+            local_m = slice((mc % 2) * P, (mc % 2 + 1) * P)
+            for b in range(2):
+                z_codes, z_scales = z_q[b, mc]
+                for n in range(N // P):
+                    codes, scales = w5_q[n // 2]
+                    local = slice(b * CHUNK + (n % 2) * P, b * CHUNK + (n % 2 + 1) * P)
+                    mx(bank[:, n * P : (n + 1) * P], codes[:, local].bitcast(FP8X4), scales[:, local],
+                       z_codes, z_scales, b == 0 and n == 0, b == 1 and n == N // P - 1)
+            if mc % 2 == 0:
+                results[mc // 2] = ring.tile([P, N // P, CHUNK], F32, name="result", tag="raw", bufs=11, align_bytes=64)
+            result = results[mc // 2]
+            nc.scalar.activation(result[:, :, local_m], bank[:].rearrange("p (n m) -> p n m", m=P), ACT.Tanh)
+            rows = out.rearrange("(n p) m -> p n m", p=P)
+            if mc >= 6:
+                nc.sync.dma_start(rows[:, :, mc * P : (mc + 1) * P], result[:, :, local_m])
+            elif mc % 2 == 1:
+                nc.sync.dma_start(rows[:, :, (mc - 1) * P : (mc + 1) * P], result[:])
+
+        steps = [("b", c) for c in range(5)] + [("a", c) for c in range(4)]
+        for c in range(4, SLICES):
+            if c + 1 < SLICES:
+                steps.append(("b", c + 1))
+            steps.append(("a", c))
+        holds = {("b", 1): "stage_w3_2", ("b", 2): "stage_w3_2", ("b", 4): "tab_sb1",
+                 ("a", 4): "tab_sb1", ("b", 6): "tab2_sb", ("a", 5): "tab_plane", ("a", 6): "tab_plane", ("a", 7): "tab_sb1"}
+        z_after = {("a", 4): 0, ("b", 6): 1, ("a", 5): 2, ("a", 7): 3}
+        products = {}
+
+        def multiply(step):
+            products[step] = quality(step[1]) if step[0] == "b" else facade(step[1])
+
+        def join(step):
+            features[step] = combine(*products[step], holds.get(step))
+
+        w3_q[0] = quantised("w3_0", [w3_raw[0]], nc.scalar.copy)
+        multiply(steps[0])
+        join(steps[0])
+        w3_q[1] = quantised("w3_1", [w3_raw[1]], nc.scalar.copy)
+        multiply(steps[1])
+        w3_q[2] = quantised("w3_2", [w3_raw[2]], nc.scalar.copy, "stage_w3_2")
+        for i, (kind, c) in enumerate(steps):
+            if i == 2:
+                for a in range(2):
+                    v_scales.append(gathered("v_scales%d" % a, tab_plane[:, a * T : (a + 1) * T], list1, U8))
+                for j in (3, 4):
+                    w3_q[j] = quantised("w3_%d" % j, [w3_raw[j]], nc.scalar.copy)
+                for j in range(H // CHUNK):
+                    w1_q[j] = quantised("w1_%d" % j, w1_raw[j], nc.scalar.copy)
+                for a in range(2):
+                    v_words.append(gathered("v_words%d" % a, tab_sb[a][:], list1, U32))
+            if i + 2 < len(steps):
+                multiply(steps[i + 2])
+            early = i + 1 < len(steps) and holds.get(steps[i + 1], 1) != holds.get(steps[i], 2)
+            if early:
+                join(steps[i + 1])
+            if kind == "b":
+                nc.vector.tensor_tensor(pages_b[c % PAGES_B][:].indirect(list4[:]), features[kind, c][:], wg2_sb[:], ALU.mult)
+            else:
+                nc.vector.tensor_tensor(pages_a[c % PAGES_A][:].indirect(list3[:]), features[kind, c][:], wg1_sb[:], ALU.mult)
+            if i + 1 < len(steps) and not early:
+                join(steps[i + 1])
+            if (kind, c) in z_after:
+                q = z_after[kind, c]
+                strengthened(0, q * CHUNK, CHUNK, holds[kind, c])
+            if (kind, c) == ("b", 0):
+                open_sum(0)
+            if (kind, c) == ("b", 7):
+                for j in range(N // CHUNK):
+                    w5_q[j] = quantised("w5_%d" % j, w5_raw[j], nc.scalar.copy, None, "wg2_sb" if j == 0 else "v2_words")
+            if kind == "b":
+                continue
+            close_sum(c)
+            if c + 1 < SLICES:
+                open_sum(c + 1)
+            if c == 0:
+                load_old(0)
+                w5_raw = [[load_rows(w5, a, j * CHUNK) for a in range(2)] for j in range(N // CHUNK)]
+                for q in range(4):
+                    weave_old(0, q)
+                load_old(1)
+            if c >= 4:
+                weave_old(1, c - 4)
+        for mc in range(T2 // P):
+            strengthened(1, mc * P, P)
+            scores(mc)

@@ -23,10 +23,16 @@ K_PASS = P * PACK
 BANK = 512
 CHUNK = 256
 SLICES = H // P
-PAGES_A = 2
+PAGE_A = (0, 1, 0, 1, 0, 1, 0, 0)
 PAGES_B = 4
 W3_WIDTHS = (128, 128, 256, 256, 256)
 W4_HEAD = 256
+SCORE_BANKS = ("second", "second", "second", "first", "second", "second", "back", "back")
+W5_AT = 3
+W5_STAGE = (None, "tab2_sb")
+W5_CODES = (None, None)
+AHEAD = 2
+OUT_WIDTHS = (256, 256, 256, 128, 128)
 
 
 def tile_list_street_change_scores_kernel(
@@ -78,8 +84,10 @@ def tile_list_street_change_scores_kernel(
         def quantised(name, raws, copy, stage_tag=None, codes_tag=None):
             each = raws[0].shape[2]
             width = len(raws) * each
-            if stage_tag:
-                stage = held(stage_tag, [P, PACK * width], BF16)
+            if stage_tag == "old_raw":
+                stage = ring.tile([P, PACK * width], BF16, name="stage", tag="old_raw", bufs=1, align_bytes=64)
+            elif stage_tag:
+                stage = held("stage_held", [P, PACK * width], BF16, stage_tag)
             else:
                 stage = ring.tile([P, PACK * width], BF16, name="stage", tag="woven", bufs=6, align_bytes=64)
             for a, raw in enumerate(raws):
@@ -96,15 +104,17 @@ def tile_list_street_change_scores_kernel(
 
         tab2_plane = cleared_plane("tab2_plane", tab2_scales)
         w4_plane = cleared_plane("w4_plane", w4_scales)
-        pages_b = [held("page_b%d" % i, [P, T2], F32) for i in range(PAGES_B)]
-        pages_a = [held("page_a%d" % i, [P, T2], F32) for i in range(PAGES_A)]
-        tab_plane = cleared_plane("tab_plane", tab_scales)
-        nc.gpsimd.memset(pages_b[0][:], 0.0)
-        w2_plane = cleared_plane("w2_plane", w2_scales)
-        ident = held("ident", [P, P], F32)
-        make_identity(nc, ident[:])
-        for page in pages_b[1:] + pages_a:
-            nc.gpsimd.memset(page[:], 0.0)
+        pages = {}
+
+        def clear_page(name):
+            pages[name] = held(name, [P, T2], F32)
+            nc.gpsimd.memset(pages[name][:], 0.0)
+
+        clear_page("page_b0")
+        tab_plane = held("tab_plane", [P, T], U8)
+        nc.gpsimd.memset(tab_plane[:].bitcast(I32), 0)
+        v_scales_moved = held("v_scales_moved", [P, S], U8)
+        nc.gpsimd.memset(v_scales_moved[:].bitcast(I32), 0)
 
         flat = "p t i -> p (t i)"
         w3_starts = [sum(W3_WIDTHS[:j]) for j in range(len(W3_WIDTHS))]
@@ -122,18 +132,12 @@ def tile_list_street_change_scores_kernel(
         w3_raw.append(load_rows(w3, 0, w3_starts[2], width=W3_WIDTHS[2]))
         w4_rest = load_words("w4_rest", w4_flat[:, 4 * W4_HEAD :], U32)
         list1 = load_list("list1", offs)
-        load_plane(tab_plane, tab_scales)
+        for q in range(4):
+            nc.sync.dma_start(tab_plane[32 * q : 32 * q + 8, :].bitcast(I32), tab_scales[:, 4 * q : 4 * q + 4, :].bitcast(I32))
         for j in (3, 4):
             w3_raw.append(load_rows(w3, 0, w3_starts[j], width=W3_WIDTHS[j]))
         w1_raw = [[load_rows(w1, a, j * CHUNK) for a in range(2)] for j in range(H // CHUNK - 1)]
         w1_raw.append([load_rows(w1, 0, H - CHUNK), load_rows(w1, 1, H - CHUNK, "raw_last", 1)])
-        load_plane(w2_plane, w2_scales)
-        w2_sb = [load_words("w2_sb%d" % a, w2_words[a], U8) for a in range(2)]
-        list3 = load_list("list3", offs3)
-        wg1_sb = held("wg1_sb", [P, S], F32)
-        nc.sync.dma_start(wg1_sb[:], wg1)
-        tab_sb = [load_words("tab_sb%d" % a, tab_words[a].rearrange(flat), U32) for a in range(2)]
-
         v2_scales = gathered("v2_scales", tab2_plane[:], list2, U8)
         v2_words = gathered("v2_words", tab2_sb[:], list2, U32)
 
@@ -147,11 +151,13 @@ def tile_list_street_change_scores_kernel(
                                 rhs_scale=rhs_scale, start=start, stop=stop)
 
         def product_bank(tag):
-            return psum.tile([P, BANK], F32, name=tag, tag=tag, bufs=1 if tag == "first" else 3)
+            return psum.tile([P, BANK], F32, name=tag, tag=tag, bufs={"first": 1, "second": 3, "back": 2}[tag])
 
-        def staged(first, second, op, late=False):
+        def staged(first, second, op, late=False, tag=None):
             if late:
                 copied = ring.tile([P, S], F32, name="copied", tag="raw_last", bufs=1, align_bytes=64)
+            elif tag:
+                copied = held("copied_held", [P, S], F32, tag)
             else:
                 copied = ring.tile([P, S], F32, name="copied", tag="copied", bufs=3)
             nc.scalar.copy(copied[:], first[:])
@@ -174,7 +180,7 @@ def tile_list_street_change_scores_kernel(
             b2, b1 = product_bank("first"), product_bank("second")
             mx(b2[:], w4_cols.bitcast(FP8X4), w4_plane[:, cols], v2_words[:], v2_scales[:], True, True)
             mx(b1[:], codes[:, local].bitcast(FP8X4), scales[:, local], v2_words[:], v2_scales[:], True, True)
-            return staged(b2, b1, ALU.mult, c == 4)
+            return staged(b2, b1, ALU.mult, c == 4, page_after.get(c))
 
         def facade(c):
             j = c // 2
@@ -182,10 +188,11 @@ def tile_list_street_change_scores_kernel(
             a2, a1 = product_bank("first"), product_bank("second")
             for a in range(2):
                 mx(a2[:], w2_sb[a][:, 2 * c * P : 2 * (c + 1) * P].bitcast(FP4X4),
-                   w2_plane[:, a * H + c * P : a * H + (c + 1) * P], v_words[a][:], v_scales[a][:], a == 0, a == 1)
+                   w2_plane[:, a * H + c * P : a * H + (c + 1) * P], v_words[a][:],
+                   v_scales_moved[:] if a else v_scales[0][:], a == 0, a == 1)
             for a in range(2):
                 local = slice(a * CHUNK + (c % 2) * P, a * CHUNK + (c % 2 + 1) * P)
-                mx(a1[:], codes[:, local].bitcast(FP8X4), scales[:, local], v_words[a][:], v_scales[a][:], a == 0, a == 1)
+                mx(a1[:], codes[:, local].bitcast(FP8X4), scales[:, local], v_words[a][:], v_scales[0][4 * a :, :], a == 0, a == 1)
             return staged(a2, a1, ALU.max)
 
         def turn(bank, page, half, start, stop):
@@ -197,7 +204,7 @@ def tile_list_street_change_scores_kernel(
         def open_sum(c):
             sums[c] = [psum.tile([P, BANK], F32, name="sum", tag="sum", bufs=2) for half in range(2)]
             for half in range(2):
-                turn(sums[c][half], pages_b[c % PAGES_B], half, True, False)
+                turn(sums[c][half], pages["page_b%d" % (c % PAGES_B)], half, True, False)
 
         def close_sum(c):
             b, quarter = divmod(c, 4)
@@ -206,13 +213,13 @@ def tile_list_street_change_scores_kernel(
                     absum[b, half] = held("absum_last", [P, 4, PACK, P], F32, "tab_sb0")
                 elif quarter == 0:
                     absum[b, half] = ring.tile([P, 4, PACK, P], F32, name="absum", tag="absum", bufs=3)
-                turn(sums[c][half], pages_a[c % PAGES_A], half, False, True)
+                turn(sums[c][half], pages["page_a%d" % PAGE_A[c]], half, False, True)
                 nc.scalar.activation(
                     absum[b, half][:, :, :, 32 * quarter : 32 * quarter + 32],
                     sums[c][half][:].rearrange("m (i q t) -> m i t q", i=4, t=PACK), ACT.Abs)
 
         def load_old(b):
-            old_raw[b] = ring.tile([P, PACK, T2], F32, name="old_raw", tag="old_raw", bufs=1)
+            old_raw[b] = ring.tile([P, PACK, T2], F32, name="old_raw", tag="old_raw", bufs=1, align_bytes=64)
             nc.sync.dma_start(old_raw[b][:], oldmap[b * K_PASS : (b + 1) * K_PASS, :].rearrange("(p t) m -> p t m", t=PACK))
 
         def weave_old(b, q):
@@ -238,39 +245,34 @@ def tile_list_street_change_scores_kernel(
             codes = held("z_codes%d_%d" % (b, m0), [P, width], U32)
             scales = held("z_scales%d_%d" % (b, m0), [P, width], U8)
             nc.vector.quantize_mx(out=codes[:].bitcast(FP8X4), scales=scales[:], in_=z[:, : PACK * width])
-            for i in range(width // P):
-                z_q[b, m0 // P + i] = (codes[:, i * P : (i + 1) * P], scales[:, i * P : (i + 1) * P])
+            z_q[b, m0 if b else m0 // CHUNK] = (codes, scales)
 
-        results = {}
-
-        def scores(mc):
-            bank = product_bank("first" if mc % 4 == 3 else "second")
-            local_m = slice((mc % 2) * P, (mc % 2 + 1) * P)
-            for b in range(2):
-                z_codes, z_scales = z_q[b, mc]
-                for n in range(N // P):
-                    codes, scales = w5_q[n // 2]
-                    local = slice(b * CHUNK + (n % 2) * P, b * CHUNK + (n % 2 + 1) * P)
-                    mx(bank[:, n * P : (n + 1) * P], codes[:, local].bitcast(FP8X4), scales[:, local],
-                       z_codes, z_scales, b == 0 and n == 0, b == 1 and n == N // P - 1)
-            if mc % 2 == 0:
-                results[mc // 2] = ring.tile([P, N // P, CHUNK], F32, name="result", tag="raw", bufs=11, align_bytes=64)
-            result = results[mc // 2]
-            nc.scalar.activation(result[:, :, local_m], bank[:].rearrange("p (n m) -> p n m", m=P), ACT.Tanh)
-            rows = out.rearrange("(n p) m -> p n m", p=P)
-            if mc >= 6:
-                nc.sync.dma_start(rows[:, :, mc * P : (mc + 1) * P], result[:, :, local_m])
-            elif mc % 2 == 1:
-                nc.sync.dma_start(rows[:, :, (mc - 1) * P : (mc + 1) * P], result[:])
+        def scores(m0, width, tags):
+            per_bank = BANK // width
+            for n0, tag in zip(range(0, N // P, per_bank), tags):
+                bank = product_bank(tag)
+                for b in range(2):
+                    z_codes, z_scales = z_q[b, m0 // CHUNK] if b == 0 else z_q[b, m0]
+                    cols = slice(m0 % CHUNK, m0 % CHUNK + width) if b == 0 else slice(0, width)
+                    for i in range(per_bank):
+                        n = n0 + i
+                        codes, scales = w5_q[n // 2]
+                        local = slice(b * CHUNK + (n % 2) * P, b * CHUNK + (n % 2 + 1) * P)
+                        mx(bank[:, i * width : (i + 1) * width], codes[:, local].bitcast(FP8X4), scales[:, local],
+                           z_codes[:, cols], z_scales[:, cols], b == 0 and i == 0, b == 1 and i == per_bank - 1)
+                result = ring.tile([P, per_bank, width], F32, name="result", tag="raw", bufs=11, align_bytes=64)
+                nc.scalar.activation(result[:], bank[:].rearrange("p (n m) -> p n m", m=width), ACT.Tanh)
+                nc.sync.dma_start(out.rearrange("(n p) m -> p n m", p=P)[:, n0 : n0 + per_bank, m0 : m0 + width], result[:])
 
         steps = [("b", c) for c in range(5)] + [("a", c) for c in range(4)]
         for c in range(4, SLICES):
             if c + 1 < SLICES:
                 steps.append(("b", c + 1))
             steps.append(("a", c))
-        holds = {("b", 1): "stage_w3_2", ("b", 2): "stage_w3_2", ("b", 4): "tab_sb1",
-                 ("a", 4): "tab_sb1", ("b", 6): "tab2_sb", ("a", 5): "tab_plane", ("a", 6): "tab_plane", ("a", 7): "tab_sb1"}
-        z_after = {("a", 4): 0, ("b", 6): 1, ("a", 5): 2, ("a", 7): 3}
+        page_after = {0: "page_b1", 1: "page_b3", 2: "page_a0", 3: "page_a1"}
+        holds = {("b", 0): "page_b2", ("b", 1): "stage_w3_2", ("b", 2): "stage_w3_2", ("b", 4): "tab_sb1",
+                 ("a", 4): "tab_sb1", ("a", 5): "tab2_sb", ("a", 6): "stage_w3_2", ("a", 7): "tab_sb1"}
+        z_after = {("a", 4): 0, ("a", 5): 1, ("a", 6): 2, ("a", 7): 3}
         products = {}
 
         def multiply(step):
@@ -278,42 +280,57 @@ def tile_list_street_change_scores_kernel(
 
         def join(step):
             features[step] = combine(*products[step], holds.get(step))
+            if step[0] == "b" and step[1] in page_after:
+                clear_page(page_after[step[1]])
 
-        w3_q[0] = quantised("w3_0", [w3_raw[0]], nc.scalar.copy)
+        w3_q[0] = quantised("w3_0", [w3_raw[0]], nc.scalar.copy, "ident")
+        ident = held("ident", [P, P], F32)
+        make_identity(nc, ident[:])
         multiply(steps[0])
         join(steps[0])
-        w3_q[1] = quantised("w3_1", [w3_raw[1]], nc.scalar.copy)
+        w3_q[1] = quantised("w3_1", [w3_raw[1]], nc.scalar.copy, "w2_plane")
+        w2_plane = cleared_plane("w2_plane", w2_scales)
+        load_plane(w2_plane, w2_scales)
+        w2_sb = [load_words("w2_sb%d" % a, w2_words[a], U8) for a in range(2)]
+        list3 = load_list("list3", offs3)
+        wg1_sb = held("wg1_sb", [P, S], F32)
+        nc.sync.dma_start(wg1_sb[:], wg1)
+        tab_sb = [load_words("tab_sb%d" % a, tab_words[a].rearrange(flat), U32) for a in range(2)]
+
         multiply(steps[1])
         w3_q[2] = quantised("w3_2", [w3_raw[2]], nc.scalar.copy, "stage_w3_2")
+        if AHEAD > 2:
+            multiply(steps[2])
+        v_scales.append(gathered("v_scales", tab_plane[:], list1, U8))
+        for q in range(4):
+            nc.gpsimd.dma_start(v_scales_moved[32 * q : 32 * q + 4, :].bitcast(I32),
+                                v_scales[0][32 * q + 4 : 32 * q + 8, :].bitcast(I32))
         for i, (kind, c) in enumerate(steps):
-            if i == 2:
-                for a in range(2):
-                    v_scales.append(gathered("v_scales%d" % a, tab_plane[:, a * T : (a + 1) * T], list1, U8))
-                for j in (3, 4):
-                    w3_q[j] = quantised("w3_%d" % j, [w3_raw[j]], nc.scalar.copy)
-                for j in range(H // CHUNK):
-                    w1_q[j] = quantised("w1_%d" % j, w1_raw[j], nc.scalar.copy)
-                for a in range(2):
-                    v_words.append(gathered("v_words%d" % a, tab_sb[a][:], list1, U32))
-            if i + 2 < len(steps):
-                multiply(steps[i + 2])
             early = i + 1 < len(steps) and holds.get(steps[i + 1], 1) != holds.get(steps[i], 2)
             if early:
                 join(steps[i + 1])
             if kind == "b":
-                nc.vector.tensor_tensor(pages_b[c % PAGES_B][:].indirect(list4[:]), features[kind, c][:], wg2_sb[:], ALU.mult)
+                nc.vector.tensor_tensor(pages["page_b%d" % (c % PAGES_B)][:].indirect(list4[:]), features[kind, c][:], wg2_sb[:], ALU.mult)
             else:
-                nc.vector.tensor_tensor(pages_a[c % PAGES_A][:].indirect(list3[:]), features[kind, c][:], wg1_sb[:], ALU.mult)
+                nc.vector.tensor_tensor(pages["page_a%d" % PAGE_A[c]][:].indirect(list3[:]), features[kind, c][:], wg1_sb[:], ALU.mult)
             if i + 1 < len(steps) and not early:
                 join(steps[i + 1])
+            if i == 0:
+                clear_page("page_b2")
+            if i == 1:
+                for j in (3, 4):
+                    w3_q[j] = quantised("w3_%d" % j, [w3_raw[j]], nc.scalar.copy)
+                for j in range(H // CHUNK):
+                    w1_q[j] = quantised("w1_%d" % j, w1_raw[j], nc.scalar.copy, "old_raw" if j == 0 else None)
+                for a in range(2):
+                    v_words.append(gathered("v_words%d" % a, tab_sb[a][:], list1, U32))
+            if i + AHEAD < len(steps):
+                multiply(steps[i + AHEAD])
             if (kind, c) in z_after:
                 q = z_after[kind, c]
                 strengthened(0, q * CHUNK, CHUNK, holds[kind, c])
             if (kind, c) == ("b", 0):
                 open_sum(0)
-            if (kind, c) == ("b", 7):
-                for j in range(N // CHUNK):
-                    w5_q[j] = quantised("w5_%d" % j, w5_raw[j], nc.scalar.copy, None, "wg2_sb" if j == 0 else "v2_words")
             if kind == "b":
                 continue
             close_sum(c)
@@ -325,8 +342,14 @@ def tile_list_street_change_scores_kernel(
                 for q in range(4):
                     weave_old(0, q)
                 load_old(1)
+            if c == W5_AT:
+                for j in range(N // CHUNK):
+                    w5_q[j] = quantised("w5_%d" % j, w5_raw[j], nc.scalar.copy, W5_STAGE[j], W5_CODES[j])
             if c >= 4:
                 weave_old(1, c - 4)
-        for mc in range(T2 // P):
-            strengthened(1, mc * P, P)
-            scores(mc)
+        m0, used = 0, 0
+        for width in OUT_WIDTHS:
+            banks = N // P * width // BANK
+            strengthened(1, m0, width)
+            scores(m0, width, [SCORE_BANKS[used + i] for i in range(banks)])
+            m0, used = m0 + width, used + banks

@@ -27,11 +27,14 @@ PAGE_A = (0, 1, 0, 1, 0, 1, 0, 0)
 PAGES_B = 4
 W3_WIDTHS = (128, 128, 256, 256, 256)
 W4_HEAD = 256
+LATE_AT = 4
+LATE_STAGE = (None, None, None)
+EARLY = 11
 SCORE_BANKS = ("second", "second", "second", "first", "second", "second", "back", "back")
 W5_AT = 3
 W5_STAGE = (None, "tab2_sb")
 W5_CODES = (None, None)
-AHEAD = 2
+AHEAD = 3
 OUT_WIDTHS = (256, 256, 256, 128, 128)
 
 
@@ -72,7 +75,7 @@ def tile_list_street_change_scores_kernel(
                     source[:, 4 * q : 4 * q + 4, :].bitcast(I32).rearrange("a r t -> r a t"),
                 )
 
-        def load_rows(source, a, c0, tag="raw", bufs=11, width=CHUNK):
+        def load_rows(source, a, c0, tag="raw", bufs=10, width=CHUNK):
             raw = ring.tile([P, PACK, width], F32, name="raw", tag=tag, bufs=bufs, align_bytes=64)
             rows = source[a * K_PASS : (a + 1) * K_PASS, c0 : c0 + width]
             nc.sync.dma_start(raw[:], rows.rearrange("(p t) c -> p t c", t=PACK))
@@ -134,10 +137,9 @@ def tile_list_street_change_scores_kernel(
         list1 = load_list("list1", offs)
         for q in range(4):
             nc.sync.dma_start(tab_plane[32 * q : 32 * q + 8, :].bitcast(I32), tab_scales[:, 4 * q : 4 * q + 4, :].bitcast(I32))
-        for j in (3, 4):
-            w3_raw.append(load_rows(w3, 0, w3_starts[j], width=W3_WIDTHS[j]))
-        w1_raw = [[load_rows(w1, a, j * CHUNK) for a in range(2)] for j in range(H // CHUNK - 1)]
-        w1_raw.append([load_rows(w1, 0, H - CHUNK), load_rows(w1, 1, H - CHUNK, "raw_last", 1)])
+        w3_raw.append(load_rows(w3, 0, w3_starts[3], width=W3_WIDTHS[3]))
+        w1_raw = [[load_rows(w1, a, 0) for a in range(2)]]
+        w1_raw.append([load_rows(w1, 0, CHUNK), load_rows(w1, 1, CHUNK, "raw_last", 1)])
         v2_scales = gathered("v2_scales", tab2_plane[:], list2, U8)
         v2_words = gathered("v2_words", tab2_sb[:], list2, U32)
 
@@ -152,6 +154,10 @@ def tile_list_street_change_scores_kernel(
 
         def product_bank(tag):
             return psum.tile([P, BANK], F32, name=tag, tag=tag, bufs={"first": 1, "second": 3, "back": 2}[tag])
+
+        def first_tag(kind, c):
+            i = steps.index((kind, c))
+            return "back" if i < EARLY and i % 3 else "first"
 
         def staged(first, second, op, late=False, tag=None):
             if late:
@@ -177,7 +183,7 @@ def tile_list_street_change_scores_kernel(
             codes, scales = w3_q[j]
             local = slice(c * P - w3_starts[j], (c + 1) * P - w3_starts[j])
             w4_cols = w4_head[:, cols] if c * P < W4_HEAD else w4_rest[:, c * P - W4_HEAD : (c + 1) * P - W4_HEAD]
-            b2, b1 = product_bank("first"), product_bank("second")
+            b2, b1 = product_bank(first_tag("b", c)), product_bank("second")
             mx(b2[:], w4_cols.bitcast(FP8X4), w4_plane[:, cols], v2_words[:], v2_scales[:], True, True)
             mx(b1[:], codes[:, local].bitcast(FP8X4), scales[:, local], v2_words[:], v2_scales[:], True, True)
             return staged(b2, b1, ALU.mult, c == 4, page_after.get(c))
@@ -185,7 +191,7 @@ def tile_list_street_change_scores_kernel(
         def facade(c):
             j = c // 2
             codes, scales = w1_q[j]
-            a2, a1 = product_bank("first"), product_bank("second")
+            a2, a1 = product_bank(first_tag("a", c)), product_bank("second")
             for a in range(2):
                 mx(a2[:], w2_sb[a][:, 2 * c * P : 2 * (c + 1) * P].bitcast(FP4X4),
                    w2_plane[:, a * H + c * P : a * H + (c + 1) * P], v_words[a][:],
@@ -224,7 +230,7 @@ def tile_list_street_change_scores_kernel(
 
         def weave_old(b, q):
             old_woven[b, q] = ring.tile([P, PACK * CHUNK], F32, name="old_woven", tag="raw" if b else "woven",
-                                        bufs=11 if b else 6, align_bytes=64)
+                                        bufs=10 if b else 6, align_bytes=64)
             weave(nc.scalar.copy, old_woven[b, q][:], old_raw[b][:, :, q * CHUNK : (q + 1) * CHUNK])
 
         def strengthened(b, m0, width, tag=None):
@@ -260,7 +266,7 @@ def tile_list_street_change_scores_kernel(
                         local = slice(b * CHUNK + (n % 2) * P, b * CHUNK + (n % 2 + 1) * P)
                         mx(bank[:, i * width : (i + 1) * width], codes[:, local].bitcast(FP8X4), scales[:, local],
                            z_codes[:, cols], z_scales[:, cols], b == 0 and i == 0, b == 1 and i == per_bank - 1)
-                result = ring.tile([P, per_bank, width], F32, name="result", tag="raw", bufs=11, align_bytes=64)
+                result = ring.tile([P, per_bank, width], F32, name="result", tag="raw", bufs=10, align_bytes=64)
                 nc.scalar.activation(result[:], bank[:].rearrange("p (n m) -> p n m", m=width), ACT.Tanh)
                 nc.sync.dma_start(out.rearrange("(n p) m -> p n m", p=P)[:, n0 : n0 + per_bank, m0 : m0 + width], result[:])
 
@@ -270,7 +276,7 @@ def tile_list_street_change_scores_kernel(
                 steps.append(("b", c + 1))
             steps.append(("a", c))
         page_after = {0: "page_b1", 1: "page_b3", 2: "page_a0", 3: "page_a1"}
-        holds = {("b", 0): "page_b2", ("b", 1): "stage_w3_2", ("b", 2): "stage_w3_2", ("b", 4): "tab_sb1",
+        holds = {("b", 0): "page_b2", ("b", 1): "stage_w3_2", ("b", 2): "stage_w3_2", ("b", 3): "tab_plane", ("b", 4): "tab_sb1",
                  ("a", 4): "tab_sb1", ("a", 5): "tab2_sb", ("a", 6): "stage_w3_2", ("a", 7): "tab_sb1"}
         z_after = {("a", 4): 0, ("a", 5): 1, ("a", 6): 2, ("a", 7): 3}
         products = {}
@@ -303,7 +309,7 @@ def tile_list_street_change_scores_kernel(
             multiply(steps[2])
         v_scales.append(gathered("v_scales", tab_plane[:], list1, U8))
         for q in range(4):
-            nc.gpsimd.dma_start(v_scales_moved[32 * q : 32 * q + 4, :].bitcast(I32),
+            nc.sync.dma_start(v_scales_moved[32 * q : 32 * q + 4, :].bitcast(I32),
                                 v_scales[0][32 * q + 4 : 32 * q + 8, :].bitcast(I32))
         for i, (kind, c) in enumerate(steps):
             early = i + 1 < len(steps) and holds.get(steps[i + 1], 1) != holds.get(steps[i], 2)
@@ -318,12 +324,15 @@ def tile_list_street_change_scores_kernel(
             if i == 0:
                 clear_page("page_b2")
             if i == 1:
-                for j in (3, 4):
-                    w3_q[j] = quantised("w3_%d" % j, [w3_raw[j]], nc.scalar.copy)
-                for j in range(H // CHUNK):
-                    w1_q[j] = quantised("w1_%d" % j, w1_raw[j], nc.scalar.copy, "old_raw" if j == 0 else None)
+                w3_q[3] = quantised("w3_3", [w3_raw[3]], nc.scalar.copy)
+                for j in range(2):
+                    w1_q[j] = quantised("w1_%d" % j, w1_raw[j], nc.scalar.copy)
                 for a in range(2):
                     v_words.append(gathered("v_words%d" % a, tab_sb[a][:], list1, U32))
+            if i == LATE_AT:
+                w1_q[2] = quantised("w1_2", [load_rows(w1, a, 2 * CHUNK) for a in range(2)], nc.scalar.copy, LATE_STAGE[0])
+                w3_q[4] = quantised("w3_4", [load_rows(w3, 0, w3_starts[4])], nc.scalar.copy, LATE_STAGE[1])
+                w1_q[3] = quantised("w1_3", [load_rows(w1, a, 3 * CHUNK) for a in range(2)], nc.scalar.copy, LATE_STAGE[2])
             if i + AHEAD < len(steps):
                 multiply(steps[i + AHEAD])
             if (kind, c) in z_after:

@@ -3,7 +3,7 @@ from contextlib import ExitStack
 import concourse.mybir as mybir
 from concourse.masks import make_identity
 
-K, K2, T, TB, S, H, T2, N = 1024, 512, 2048, 1024, 512, 1024, 1024, 512
+K, K2, T, S, H, T2, N = 1024, 512, 2048, 512, 1024, 1024, 512
 FLOPS = 2 * S * H * (2 * K + 2 * K2) + 2 * H * N * T2
 
 F32 = mybir.dt.float32
@@ -20,22 +20,22 @@ ACT = mybir.ActivationFunctionType
 P = 128
 PACK = 4
 K_PASS = P * PACK
+QUADRANT = 32
 BANK = 512
 CHUNK = 256
 SLICES = H // P
-PAGE_A = (0, 1, 0, 1, 0, 1, 0, 0)
+LAST = SLICES - 1
+SLICES_PER_PASS = K_PASS // P
+
+B_BEFORE = 4
 PAGES_B = 4
+AHEAD = 3
 W3_WIDTHS = (128, 128, 256, 256, 256)
 W4_HEAD = 256
-LATE_AT = 4
-LATE_STAGE = (None, None, None)
-EARLY = 11
-SCORE_BANKS = ("second", "second", "second", "first", "second", "second", "back", "back")
-W5_AT = 3
-W5_STAGE = (None, "tab2_sb")
-W5_CODES = (None, None)
-AHEAD = 3
 OUT_WIDTHS = (256, 256, 256, 128, 128)
+RING_BUFS = {"raw": 10, "woven": 6, "copied": 3, "feature": 3, "magnitude": 3, "z": 3, "old_rows": 1, "w1_early_end": 1}
+PSUM_BUFS = {"first": 1, "second": 3, "sum": 2, "back": 2}
+SCORE_BANKS = ("second", "second", "second", "first", "second", "second", "sum", "sum")
 
 
 def tile_list_street_change_scores_kernel(
@@ -45,320 +45,297 @@ def tile_list_street_change_scores_kernel(
     nc = tc.nc
     with ExitStack() as ctx:
         keep = ctx.enter_context(tc.tile_pool(name="keep", bufs=1))
-        ring = ctx.enter_context(tc.tile_pool(name="ring", bufs=2))
-        psum = ctx.enter_context(tc.psum_pool(name="psum", bufs=2))
+        ring = ctx.enter_context(tc.tile_pool(name="ring", bufs=1))
+        psum = ctx.enter_context(tc.psum_pool(name="psum", bufs=1))
 
-        def held(name, shape, dtype, tag=None):
-            return keep.tile(shape, dtype, name=name, tag=tag or name, align_bytes=64)
+        def sbuf(name, shape, dtype, slot=None):
+            slot = slot or name
+            if slot in RING_BUFS:
+                return ring.tile(shape, dtype, name=name, tag=slot, bufs=RING_BUFS[slot], align_bytes=64)
+            return keep.tile(shape, dtype, name=name, tag=slot, align_bytes=64)
 
-        def load_list(name, source):
-            tile = held(name, [P, S // 16], U16)
+        def bank(tag, shape=(P, BANK)):
+            return psum.tile(list(shape), F32, name=tag, tag=tag, bufs=PSUM_BUFS[tag])
+
+        def load(name, source, dtype):
+            tile = sbuf(name, list(source.shape), dtype)
             nc.sync.dma_start(tile[:], source)
             return tile
 
         def load_words(name, source, dtype):
-            width = source.shape[1] if dtype == U8 else source.shape[1] // 4
-            tile = held(name, [P, width], dtype)
+            tile = sbuf(name, [P, source.shape[1] // (1 if dtype == U8 else PACK)], dtype)
             nc.sync.dma_start(tile[:].bitcast(I32), source.bitcast(I32))
             return tile
 
-        def cleared_plane(name, source):
-            tile = held(name, [P, source.shape[0] * source.shape[2]], U8)
-            nc.gpsimd.memset(tile[:].bitcast(I32), 0)
-            return tile
+        def cleared_plane(name, width):
+            plane = sbuf(name, [P, width], U8)
+            nc.gpsimd.memset(plane[:].bitcast(I32), 0)
+            return plane
 
-        def load_plane(tile, source):
-            passes = source.shape[0]
-            for q in range(4):
+        def load_plane(plane, source):
+            for q in range(P // QUADRANT):
                 nc.sync.dma_start(
-                    tile[32 * q : 32 * q + 4, :].bitcast(I32).rearrange("r (a t) -> r a t", a=passes),
+                    plane[QUADRANT * q : QUADRANT * q + 4, :].bitcast(I32).rearrange("r (a t) -> r a t", a=source.shape[0]),
                     source[:, 4 * q : 4 * q + 4, :].bitcast(I32).rearrange("a r t -> r a t"),
                 )
 
-        def load_rows(source, a, c0, tag="raw", bufs=10, width=CHUNK):
-            raw = ring.tile([P, PACK, width], F32, name="raw", tag=tag, bufs=bufs, align_bytes=64)
-            rows = source[a * K_PASS : (a + 1) * K_PASS, c0 : c0 + width]
-            nc.sync.dma_start(raw[:], rows.rearrange("(p t) c -> p t c", t=PACK))
-            return raw
+        def load_rows(source, a, c0, width=CHUNK, slot="raw"):
+            rows = sbuf("rows", [P, PACK, width], F32, slot)
+            block = source[a * K_PASS : (a + 1) * K_PASS, c0 : c0 + width]
+            nc.sync.dma_start(rows[:], block.rearrange("(p t) c -> p t c", t=PACK))
+            return rows
 
-        def weave(copy, dst, src):
-            copy(dst.rearrange("p (c i t) -> p c t i", i=2, t=PACK), src.rearrange("p t (c i) -> p c t i", i=2))
+        def weave(dst, src):
+            nc.scalar.copy(dst.rearrange("p (c i t) -> p c t i", i=4, t=PACK), src.rearrange("p t (c i) -> p c t i", i=4))
 
-        def quantised(name, raws, copy, stage_tag=None, codes_tag=None):
-            each = raws[0].shape[2]
-            width = len(raws) * each
-            if stage_tag == "old_raw":
-                stage = ring.tile([P, PACK * width], BF16, name="stage", tag="old_raw", bufs=1, align_bytes=64)
-            elif stage_tag:
-                stage = held("stage_held", [P, PACK * width], BF16, stage_tag)
-            else:
-                stage = ring.tile([P, PACK * width], BF16, name="stage", tag="woven", bufs=6, align_bytes=64)
-            for a, raw in enumerate(raws):
-                weave(copy, stage[:, a * PACK * each : (a + 1) * PACK * each], raw[:])
-            codes = held(name + "_codes", [P, width], U32, codes_tag)
-            scales = held(name + "_scales", [P, width], U8)
-            nc.vector.quantize_mx(out=codes[:].bitcast(FP8X4), scales=scales[:], in_=stage[:])
-            return codes, scales
+        def staged(passes, slot="woven"):
+            size = PACK * passes[0].shape[2]
+            stage = sbuf("stage", [P, len(passes) * size], BF16, slot)
+            for a, rows in enumerate(passes):
+                weave(stage[:, a * size : (a + 1) * size], rows[:])
+            return stage
+
+        def quantised(name, values):
+            width = values.shape[1] // PACK
+            codes = sbuf(name + "_codes", [P, width], U32)
+            plane = sbuf(name + "_plane", [P, width], U8)
+            nc.vector.quantize_mx(out=codes[:].bitcast(FP8X4), scales=plane[:], in_=values)
+            return codes, plane
 
         def gathered(name, window, offsets, dtype):
-            tile = held(name, [P, S], dtype)
-            nc.vector.tensor_copy(tile[:], window.indirect(offsets[:]))
+            tile = sbuf(name, [P, S], dtype)
+            nc.vector.tensor_copy(tile[:], window[:].indirect(offsets[:]))
             return tile
 
-        tab2_plane = cleared_plane("tab2_plane", tab2_scales)
-        w4_plane = cleared_plane("w4_plane", w4_scales)
+        def mx(result, lhs, lhs_plane, rhs, rhs_plane, start, stop):
+            nc.tensor.matmul_mx(out=result, lhsT=lhs, lhsT_scale=lhs_plane, rhs=rhs.bitcast(FP8X4),
+                                rhs_scale=rhs_plane, start=start, stop=stop)
+
         pages = {}
 
-        def clear_page(name):
-            pages[name] = held(name, [P, T2], F32)
-            nc.gpsimd.memset(pages[name][:], 0.0)
+        def clear_page(kind, i, slot):
+            pages[kind, i] = sbuf("page_%s%d" % (kind, i), [P, T2], F32, slot)
+            nc.gpsimd.memset(pages[kind, i][:], 0.0)
 
-        clear_page("page_b0")
-        tab_plane = held("tab_plane", [P, T], U8)
-        nc.gpsimd.memset(tab_plane[:].bitcast(I32), 0)
-        v_scales_moved = held("v_scales_moved", [P, S], U8)
-        nc.gpsimd.memset(v_scales_moved[:].bitcast(I32), 0)
+        def page_of(kind, c):
+            if kind == "b":
+                return pages[kind, c % PAGES_B]
+            return pages[kind, min(c, LAST - 1) % 2]
 
-        flat = "p t i -> p (t i)"
+        steps = [("b", c) for c in range(B_BEFORE + 1)] + [("a", c) for c in range(B_BEFORE)]
+        for c in range(B_BEFORE, SLICES):
+            steps.extend([("b", c + 1), ("a", c)] if c < LAST else [("a", c)])
+
+        feature_slot = {("b", 0): "page_b2", ("b", 1): "w3_third", ("b", 2): "w3_third", ("b", 3): "b2_copied",
+                        ("b", B_BEFORE): "tab_sb1",
+                        ("a", 4): "tab_sb1", ("a", 5): "tab2_sb", ("a", 6): "w3_third", ("a", 7): "tab_sb1"}
+        copied_slot = {("b", 1): "ident", ("b", 2): "b2_copied", ("b", 3): "page_a0", ("b", B_BEFORE): "w1_early_end"}
+        first_pass_done = steps.index(("a", SLICES_PER_PASS))
+
+        tab2_plane = cleared_plane("tab2_plane", tab2_scales.shape[2])
+        w4_plane = cleared_plane("w4_plane", H)
+        tab_plane = cleared_plane("tab_plane", T)
+        v_plane1 = cleared_plane("v_plane1", S)
+        w2_plane = cleared_plane("w2_plane", 2 * H)
+
+        as_bytes = "p c i -> p (c i)"
         w3_starts = [sum(W3_WIDTHS[:j]) for j in range(len(W3_WIDTHS))]
-        w4_flat = w4_words[0].rearrange(flat)
-        list2 = load_list("list2", offs2)
+        w4_bytes = w4_words[0].rearrange(as_bytes)
+        list2 = load("list2", offs2, U16)
         load_plane(tab2_plane, tab2_scales)
-        tab2_sb = load_words("tab2_sb", tab2_words[0].rearrange(flat), U32)
-        w3_raw = [load_rows(w3, 0, 0, width=W3_WIDTHS[0])]
-        w4_head = load_words("w4_head", w4_flat[:, : 4 * W4_HEAD], U32)
+        tab2_sb = load_words("tab2_sb", tab2_words[0].rearrange(as_bytes), U32)
+        w3_rows = [load_rows(w3, 0, 0, W3_WIDTHS[0])]
+        w4_head = load_words("w4_head", w4_bytes[:, : PACK * W4_HEAD], U32)
         load_plane(w4_plane, w4_scales)
-        w3_raw.append(load_rows(w3, 0, w3_starts[1], width=W3_WIDTHS[1]))
-        list4 = load_list("list4", offs4)
-        wg2_sb = held("wg2_sb", [P, S], F32)
-        nc.sync.dma_start(wg2_sb[:], wg2)
-        w3_raw.append(load_rows(w3, 0, w3_starts[2], width=W3_WIDTHS[2]))
-        w4_rest = load_words("w4_rest", w4_flat[:, 4 * W4_HEAD :], U32)
-        list1 = load_list("list1", offs)
-        for q in range(4):
-            nc.sync.dma_start(tab_plane[32 * q : 32 * q + 8, :].bitcast(I32), tab_scales[:, 4 * q : 4 * q + 4, :].bitcast(I32))
-        w3_raw.append(load_rows(w3, 0, w3_starts[3], width=W3_WIDTHS[3]))
-        w1_raw = [[load_rows(w1, a, 0) for a in range(2)]]
-        w1_raw.append([load_rows(w1, 0, CHUNK), load_rows(w1, 1, CHUNK, "raw_last", 1)])
-        v2_scales = gathered("v2_scales", tab2_plane[:], list2, U8)
-        v2_words = gathered("v2_words", tab2_sb[:], list2, U32)
+        w3_rows.append(load_rows(w3, 0, w3_starts[1], W3_WIDTHS[1]))
+        list4 = load("list4", offs4, U16)
+        wg2_sb = load("wg2_sb", wg2, F32)
+        w3_rows.append(load_rows(w3, 0, w3_starts[2]))
+        w4_rest = load_words("w4_rest", w4_bytes[:, PACK * W4_HEAD :], U32)
+        list1 = load("list1", offs, U16)
+        for q in range(P // QUADRANT):
+            nc.sync.dma_start(tab_plane[QUADRANT * q : QUADRANT * q + 8, :].bitcast(I32),
+                              tab_scales[:, 4 * q : 4 * q + 4, :].bitcast(I32))
+        w3_rows.append(load_rows(w3, 0, w3_starts[3]))
+        w1_early = [[load_rows(w1, a, 0) for a in range(2)],
+                    [load_rows(w1, 0, CHUNK), load_rows(w1, 1, CHUNK, slot="w1_early_end")]]
+        v2_plane = gathered("v2_plane", tab2_plane, list2, U8)
+        v2_words = gathered("v2_words", tab2_sb, list2, U32)
 
-        w3_q, w1_q, w5_q = {}, {}, {}
-        v_words, v_scales = [], []
-        old_raw, old_woven, sums, absum, features = {}, {}, {}, {}, {}
-        z_q = {}
+        w3_mx, w1_mx, w5_mx, z_mx = {}, {}, {}, {}
+        v_words, w5_stages, ident = [], [], []
+        products, features, sums, magnitudes, old_rows, old_woven = {}, {}, {}, {}, {}, {}
 
-        def mx(bank, lhs, lhs_scale, rhs, rhs_scale, start, stop):
-            nc.tensor.matmul_mx(out=bank, lhsT=lhs, lhsT_scale=lhs_scale, rhs=rhs.bitcast(FP8X4),
-                                rhs_scale=rhs_scale, start=start, stop=stop)
-
-        def product_bank(tag):
-            return psum.tile([P, BANK], F32, name=tag, tag=tag, bufs={"first": 1, "second": 3, "back": 2}[tag])
-
-        def first_tag(kind, c):
-            i = steps.index((kind, c))
-            return "back" if i < EARLY and i % 3 else "first"
-
-        def staged(first, second, op, late=False, tag=None):
-            if late:
-                copied = ring.tile([P, S], F32, name="copied", tag="raw_last", bufs=1, align_bytes=64)
-            elif tag:
-                copied = held("copied_held", [P, S], F32, tag)
+        def multiply(step):
+            kind, c = step
+            i = steps.index(step)
+            first = bank("back" if i <= first_pass_done and i % 3 else "first")
+            second = bank("second")
+            if kind == "b":
+                j = max(n for n, start in enumerate(w3_starts) if start <= c * P)
+                local = slice(c * P - w3_starts[j], (c + 1) * P - w3_starts[j])
+                w4_cols = w4_head[:, c * P : (c + 1) * P] if c * P < W4_HEAD else w4_rest[:, c * P - W4_HEAD : (c + 1) * P - W4_HEAD]
+                weights = [(w4_cols, w4_plane[:, c * P : (c + 1) * P]), (w3_mx[j][0][:, local], w3_mx[j][1][:, local])]
+                for result, (codes, plane) in zip((first, second), weights if c else weights[::-1]):
+                    mx(result[:], codes.bitcast(FP8X4), plane, v2_words[:], v2_plane[:], True, True)
             else:
-                copied = ring.tile([P, S], F32, name="copied", tag="copied", bufs=3)
+                for a in range(2):
+                    mx(first[:], w2_sb[a][:, 2 * c * P : 2 * (c + 1) * P].bitcast(FP4X4),
+                       w2_plane[:, a * H + c * P : a * H + (c + 1) * P], v_words[a][:],
+                       (v_plane, v_plane1)[a][:], a == 0, a == 1)
+                codes, plane = w1_mx[c * P // CHUNK]
+                for a in range(2):
+                    local = slice(a * CHUNK + c * P % CHUNK, a * CHUNK + c * P % CHUNK + P)
+                    mx(second[:], codes[:, local].bitcast(FP8X4), plane[:, local], v_words[a][:], v_plane[4 * a :, :],
+                       a == 0, a == 1)
+            copied = sbuf("copy_of_first", [P, S], F32, copied_slot.get(step, "copied"))
             nc.scalar.copy(copied[:], first[:])
-            return copied, second, op
+            products[step] = (copied, second)
 
-        def combine(copied, second, op, tag=None):
-            if tag:
-                feature = held("feature_held", [P, S], F32, tag)
-            else:
-                feature = ring.tile([P, S], F32, name="feature", tag="feature", bufs=3)
-            nc.vector.tensor_tensor(feature[:], second[:], copied[:], op)
-            return feature
+        def join(step):
+            copied, second = products[step]
+            features[step] = sbuf("feature_of_step", [P, S], F32, feature_slot.get(step, "feature"))
+            nc.vector.tensor_tensor(features[step][:], second[:], copied[:], ALU.mult if step[0] == "b" else ALU.max)
+            if step == ("b", 1):
+                ident.append(sbuf("ident", [P, P], F32))
+                make_identity(nc, ident[0][:])
+            if step == ("b", 3):
+                clear_page("a", 0, copied_slot[step])
+            if step == ("b", B_BEFORE):
+                clear_page("a", 1, copied_slot[step])
 
-        def quality(c):
-            cols = slice(c * P, (c + 1) * P)
-            j = max(i for i, start in enumerate(w3_starts) if start <= c * P)
-            codes, scales = w3_q[j]
-            local = slice(c * P - w3_starts[j], (c + 1) * P - w3_starts[j])
-            w4_cols = w4_head[:, cols] if c * P < W4_HEAD else w4_rest[:, c * P - W4_HEAD : (c + 1) * P - W4_HEAD]
-            b2, b1 = product_bank(first_tag("b", c)), product_bank("second")
-            mx(b2[:], w4_cols.bitcast(FP8X4), w4_plane[:, cols], v2_words[:], v2_scales[:], True, True)
-            mx(b1[:], codes[:, local].bitcast(FP8X4), scales[:, local], v2_words[:], v2_scales[:], True, True)
-            return staged(b2, b1, ALU.mult, c == 4, page_after.get(c))
+        def place(step):
+            offsets, weight = (list4, wg2_sb) if step[0] == "b" else (list3, wg1_sb)
+            nc.vector.tensor_tensor(page_of(*step)[:].indirect(offsets[:]), features[step][:], weight[:], ALU.mult)
 
-        def facade(c):
-            j = c // 2
-            codes, scales = w1_q[j]
-            a2, a1 = product_bank(first_tag("a", c)), product_bank("second")
-            for a in range(2):
-                mx(a2[:], w2_sb[a][:, 2 * c * P : 2 * (c + 1) * P].bitcast(FP4X4),
-                   w2_plane[:, a * H + c * P : a * H + (c + 1) * P], v_words[a][:],
-                   v_scales_moved[:] if a else v_scales[0][:], a == 0, a == 1)
-            for a in range(2):
-                local = slice(a * CHUNK + (c % 2) * P, a * CHUNK + (c % 2 + 1) * P)
-                mx(a1[:], codes[:, local].bitcast(FP8X4), scales[:, local], v_words[a][:], v_scales[0][4 * a :, :], a == 0, a == 1)
-            return staged(a2, a1, ALU.max)
-
-        def turn(bank, page, half, start, stop):
+        def turn(result, page, half, start, stop):
             for i in range(4):
                 m0 = (4 * half + i) * P
-                nc.tensor.matmul(bank[:, i * P : (i + 1) * P], page[:, m0 : m0 + P], ident[:],
+                nc.tensor.matmul(result[:, i * P : (i + 1) * P], page[:, m0 : m0 + P], ident[0][:],
                                  start=start and i == 0, stop=stop and i == 3, is_transpose=True)
 
         def open_sum(c):
-            sums[c] = [psum.tile([P, BANK], F32, name="sum", tag="sum", bufs=2) for half in range(2)]
+            sums[c] = [bank(tag) for tag in (("first", "second") if c == LAST else ("sum", "sum"))]
             for half in range(2):
-                turn(sums[c][half], pages["page_b%d" % (c % PAGES_B)], half, True, False)
+                turn(sums[c][half], page_of("b", c), half, True, False)
 
         def close_sum(c):
-            b, quarter = divmod(c, 4)
+            b, quarter = divmod(c, SLICES_PER_PASS)
             for half in range(2):
-                if quarter == 0 and (b, half) == (1, 1):
-                    absum[b, half] = held("absum_last", [P, 4, PACK, P], F32, "tab_sb0")
-                elif quarter == 0:
-                    absum[b, half] = ring.tile([P, 4, PACK, P], F32, name="absum", tag="absum", bufs=3)
-                turn(sums[c][half], pages["page_a%d" % PAGE_A[c]], half, False, True)
-                nc.scalar.activation(
-                    absum[b, half][:, :, :, 32 * quarter : 32 * quarter + 32],
-                    sums[c][half][:].rearrange("m (i q t) -> m i t q", i=4, t=PACK), ACT.Abs)
+                if quarter == 0:
+                    slot = "tab_sb0" if (b, half) == (1, 1) else "magnitude"
+                    magnitudes[b, half] = sbuf("magnitude_of_half", [P, 4, PACK, P], F32, slot)
+                turn(sums[c][half], page_of("a", c), half, False, True)
+                nc.scalar.activation(magnitudes[b, half][:, :, :, QUADRANT * quarter : QUADRANT * (quarter + 1)],
+                                     sums[c][half][:].rearrange("m (i q t) -> m i t q", i=4, t=PACK), ACT.Abs)
 
-        def load_old(b):
-            old_raw[b] = ring.tile([P, PACK, T2], F32, name="old_raw", tag="old_raw", bufs=1, align_bytes=64)
-            nc.sync.dma_start(old_raw[b][:], oldmap[b * K_PASS : (b + 1) * K_PASS, :].rearrange("(p t) m -> p t m", t=PACK))
+        def weave_old(b, j):
+            old_woven[b, j] = sbuf("old_woven", [P, PACK * CHUNK], F32, ("woven", "raw")[b])
+            weave(old_woven[b, j][:], old_rows[b][:, :, j * CHUNK : (j + 1) * CHUNK])
 
-        def weave_old(b, q):
-            old_woven[b, q] = ring.tile([P, PACK * CHUNK], F32, name="old_woven", tag="raw" if b else "woven",
-                                        bufs=10 if b else 6, align_bytes=64)
-            weave(nc.scalar.copy, old_woven[b, q][:], old_raw[b][:, :, q * CHUNK : (q + 1) * CHUNK])
-
-        def strengthened(b, m0, width, tag=None):
-            if tag:
-                z = held("z_on_" + tag, [P, PACK * CHUNK], BF16, tag)
-            else:
-                z = ring.tile([P, PACK * CHUNK], BF16, name="z", tag="z", bufs=3, align_bytes=64)
+        def strengthen(b, m0, width, slot="z"):
+            z = sbuf("z_values", [P, PACK * CHUNK], BF16, slot)
             for i in range(width // P):
-                mc = m0 // P + i
-                back = psum.tile([P, PACK, P], F32, name="back", tag="sum" if b == 1 and mc % 4 >= 2 else "back", bufs=2)
+                block = m0 // P + i
+                back = bank("sum" if b == 1 and block % 4 < 2 else "back", (P, PACK, P))
                 for t in range(PACK):
-                    nc.tensor.transpose(back[:, t, :], absum[b, mc // 4][:, mc % 4, t, :], ident[:])
-                part = slice((mc % 2) * BANK, (mc % 2 + 1) * BANK)
+                    nc.tensor.transpose(back[:, t, :], magnitudes[b, block // 4][:, block % 4, t, :], ident[0][:])
+                old = old_woven[b, block // 2][:, (block % 2) * BANK : (block % 2 + 1) * BANK]
                 nc.vector.scalar_tensor_tensor(
                     z[:, i * BANK : (i + 1) * BANK].rearrange("p (m t) -> p m t", t=PACK),
-                    back[:].rearrange("p t m -> p m t"), 1.0,
-                    old_woven[b, mc // 2][:, part].rearrange("p (m t) -> p m t", t=PACK), ALU.add, ALU.mult)
-            codes = held("z_codes%d_%d" % (b, m0), [P, width], U32)
-            scales = held("z_scales%d_%d" % (b, m0), [P, width], U8)
-            nc.vector.quantize_mx(out=codes[:].bitcast(FP8X4), scales=scales[:], in_=z[:, : PACK * width])
-            z_q[b, m0 if b else m0 // CHUNK] = (codes, scales)
+                    back[:].rearrange("p t m -> p m t"), 1.0, old.rearrange("p (m t) -> p m t", t=PACK), ALU.add, ALU.mult)
+            codes, plane = quantised("z%d_%d" % (b, m0), z[:, : PACK * width])
+            for i in range(width // P):
+                z_mx[b, m0 + i * P] = (codes[:, i * P :], plane[:, i * P :])
 
-        def scores(m0, width, tags):
+        def score(m0, width, tags):
             per_bank = BANK // width
             for n0, tag in zip(range(0, N // P, per_bank), tags):
-                bank = product_bank(tag)
+                sums_n = bank(tag)
                 for b in range(2):
-                    z_codes, z_scales = z_q[b, m0 // CHUNK] if b == 0 else z_q[b, m0]
-                    cols = slice(m0 % CHUNK, m0 % CHUNK + width) if b == 0 else slice(0, width)
+                    z_codes, z_plane = z_mx[b, m0]
                     for i in range(per_bank):
-                        n = n0 + i
-                        codes, scales = w5_q[n // 2]
-                        local = slice(b * CHUNK + (n % 2) * P, b * CHUNK + (n % 2 + 1) * P)
-                        mx(bank[:, i * width : (i + 1) * width], codes[:, local].bitcast(FP8X4), scales[:, local],
-                           z_codes[:, cols], z_scales[:, cols], b == 0 and i == 0, b == 1 and i == per_bank - 1)
-                result = ring.tile([P, per_bank, width], F32, name="result", tag="raw", bufs=10, align_bytes=64)
-                nc.scalar.activation(result[:], bank[:].rearrange("p (n m) -> p n m", m=width), ACT.Tanh)
+                        codes, plane = w5_mx[(n0 + i) * P // CHUNK]
+                        c0 = b * CHUNK + (n0 + i) * P % CHUNK
+                        mx(sums_n[:, i * width : (i + 1) * width], codes[:, c0 : c0 + P].bitcast(FP8X4), plane[:, c0 : c0 + P],
+                           z_codes[:, :width], z_plane[:, :width], b == 0 and i == 0, b == 1 and i == per_bank - 1)
+                result = sbuf("result", [P, per_bank, width], F32, "raw")
+                nc.scalar.activation(result[:], sums_n[:].rearrange("p (n m) -> p n m", m=width), ACT.Tanh)
                 nc.sync.dma_start(out.rearrange("(n p) m -> p n m", p=P)[:, n0 : n0 + per_bank, m0 : m0 + width], result[:])
 
-        steps = [("b", c) for c in range(5)] + [("a", c) for c in range(4)]
-        for c in range(4, SLICES):
-            if c + 1 < SLICES:
-                steps.append(("b", c + 1))
-            steps.append(("a", c))
-        page_after = {0: "page_b1", 1: "page_b3", 2: "page_a0", 3: "page_a1"}
-        holds = {("b", 0): "page_b2", ("b", 1): "stage_w3_2", ("b", 2): "stage_w3_2", ("b", 3): "tab_plane", ("b", 4): "tab_sb1",
-                 ("a", 4): "tab_sb1", ("a", 5): "tab2_sb", ("a", 6): "stage_w3_2", ("a", 7): "tab_sb1"}
-        z_after = {("a", 4): 0, ("a", 5): 1, ("a", 6): 2, ("a", 7): 3}
-        products = {}
-
-        def multiply(step):
-            products[step] = quality(step[1]) if step[0] == "b" else facade(step[1])
-
-        def join(step):
-            features[step] = combine(*products[step], holds.get(step))
-            if step[0] == "b" and step[1] in page_after:
-                clear_page(page_after[step[1]])
-
-        w3_q[0] = quantised("w3_0", [w3_raw[0]], nc.scalar.copy, "ident")
-        ident = held("ident", [P, P], F32)
-        make_identity(nc, ident[:])
+        w3_mx[0] = quantised("w3_0", staged([w3_rows[0]], "page_b0")[:])
+        clear_page("b", 0, "page_b0")
         multiply(steps[0])
         join(steps[0])
-        w3_q[1] = quantised("w3_1", [w3_raw[1]], nc.scalar.copy, "w2_plane")
-        w2_plane = cleared_plane("w2_plane", w2_scales)
+        w3_mx[1] = quantised("w3_1", staged([w3_rows[1]], "page_b1")[:])
+        clear_page("b", 1, "page_b1")
         load_plane(w2_plane, w2_scales)
         w2_sb = [load_words("w2_sb%d" % a, w2_words[a], U8) for a in range(2)]
-        list3 = load_list("list3", offs3)
-        wg1_sb = held("wg1_sb", [P, S], F32)
-        nc.sync.dma_start(wg1_sb[:], wg1)
-        tab_sb = [load_words("tab_sb%d" % a, tab_words[a].rearrange(flat), U32) for a in range(2)]
-
+        list3 = load("list3", offs3, U16)
+        wg1_sb = load("wg1_sb", wg1, F32)
+        tab_sb = [load_words("tab_sb%d" % a, tab_words[a].rearrange(as_bytes), U32) for a in range(2)]
         multiply(steps[1])
-        w3_q[2] = quantised("w3_2", [w3_raw[2]], nc.scalar.copy, "stage_w3_2")
-        if AHEAD > 2:
-            multiply(steps[2])
-        v_scales.append(gathered("v_scales", tab_plane[:], list1, U8))
-        for q in range(4):
-            nc.sync.dma_start(v_scales_moved[32 * q : 32 * q + 4, :].bitcast(I32),
-                                v_scales[0][32 * q + 4 : 32 * q + 8, :].bitcast(I32))
-        for i, (kind, c) in enumerate(steps):
-            early = i + 1 < len(steps) and holds.get(steps[i + 1], 1) != holds.get(steps[i], 2)
-            if early:
-                join(steps[i + 1])
-            if kind == "b":
-                nc.vector.tensor_tensor(pages["page_b%d" % (c % PAGES_B)][:].indirect(list4[:]), features[kind, c][:], wg2_sb[:], ALU.mult)
-            else:
-                nc.vector.tensor_tensor(pages["page_a%d" % PAGE_A[c]][:].indirect(list3[:]), features[kind, c][:], wg1_sb[:], ALU.mult)
-            if i + 1 < len(steps) and not early:
-                join(steps[i + 1])
-            if i == 0:
-                clear_page("page_b2")
-            if i == 1:
-                w3_q[3] = quantised("w3_3", [w3_raw[3]], nc.scalar.copy)
-                for j in range(2):
-                    w1_q[j] = quantised("w1_%d" % j, w1_raw[j], nc.scalar.copy)
-                for a in range(2):
-                    v_words.append(gathered("v_words%d" % a, tab_sb[a][:], list1, U32))
-            if i == LATE_AT:
-                w1_q[2] = quantised("w1_2", [load_rows(w1, a, 2 * CHUNK) for a in range(2)], nc.scalar.copy, LATE_STAGE[0])
-                w3_q[4] = quantised("w3_4", [load_rows(w3, 0, w3_starts[4])], nc.scalar.copy, LATE_STAGE[1])
-                w1_q[3] = quantised("w1_3", [load_rows(w1, a, 3 * CHUNK) for a in range(2)], nc.scalar.copy, LATE_STAGE[2])
+        w3_mx[2] = quantised("w3_2", staged([w3_rows[2]], "w3_third")[:])
+        multiply(steps[2])
+        v_plane = gathered("v_plane", tab_plane, list1, U8)
+        clear_page("b", 3, "tab_plane")
+        for q in range(P // QUADRANT):
+            nc.sync.dma_start(v_plane1[QUADRANT * q : QUADRANT * q + 4, :].bitcast(I32),
+                              v_plane[QUADRANT * q + 4 : QUADRANT * q + 8, :].bitcast(I32))
+
+        for i, step in enumerate(steps):
+            kind, c = step
+            following = steps[i + 1 : i + 2]
+            same_slot = [s for s in following if step in feature_slot and feature_slot.get(s) == feature_slot[step]]
+            for s in following:
+                if s not in same_slot:
+                    join(s)
+            place(step)
+            for s in same_slot:
+                join(s)
+            if step == ("b", 0):
+                clear_page("b", 2, feature_slot[step])
+            if step == ("b", 1):
+                w3_mx[3] = quantised("w3_3", staged([w3_rows[3]])[:])
+                for j, passes in enumerate(w1_early):
+                    w1_mx[j] = quantised("w1_%d" % j, staged(passes)[:])
+                v_words.extend(gathered("v_words%d" % a, tab_sb[a], list1, U32) for a in range(2))
+            if step == ("b", B_BEFORE):
+                w1_mx[2] = quantised("w1_2", staged([load_rows(w1, a, 2 * CHUNK) for a in range(2)])[:])
+                w3_mx[4] = quantised("w3_4", staged([load_rows(w3, 0, w3_starts[4])])[:])
+                w1_mx[3] = quantised("w1_3", staged([load_rows(w1, a, 3 * CHUNK) for a in range(2)])[:])
             if i + AHEAD < len(steps):
                 multiply(steps[i + AHEAD])
-            if (kind, c) in z_after:
-                q = z_after[kind, c]
-                strengthened(0, q * CHUNK, CHUNK, holds[kind, c])
-            if (kind, c) == ("b", 0):
-                open_sum(0)
+            if step == ("a", LAST):
+                w5_codes = sbuf("w5_codes", [P, 2 * N], U32, "wg1_sb")
+                w5_plane = sbuf("w5_plane", [P, 2 * N], U8)
+                for j, stage in enumerate(w5_stages):
+                    cols = slice(j * N, (j + 1) * N)
+                    nc.vector.quantize_mx(out=w5_codes[:, cols].bitcast(FP8X4), scales=w5_plane[:, cols], in_=stage[:])
+                    w5_mx[j] = (w5_codes[:, cols], w5_plane[:, cols])
+            if kind == "a" and c >= SLICES_PER_PASS:
+                strengthen(0, (c - SLICES_PER_PASS) * CHUNK, CHUNK, feature_slot[step])
+            if step in (("b", 0), ("b", LAST)):
+                open_sum(c)
             if kind == "b":
                 continue
             close_sum(c)
-            if c + 1 < SLICES:
+            if c + 1 < LAST:
                 open_sum(c + 1)
             if c == 0:
-                load_old(0)
-                w5_raw = [[load_rows(w5, a, j * CHUNK) for a in range(2)] for j in range(N // CHUNK)]
-                for q in range(4):
-                    weave_old(0, q)
-                load_old(1)
-            if c == W5_AT:
-                for j in range(N // CHUNK):
-                    w5_q[j] = quantised("w5_%d" % j, w5_raw[j], nc.scalar.copy, W5_STAGE[j], W5_CODES[j])
-            if c >= 4:
-                weave_old(1, c - 4)
-        m0, used = 0, 0
+                old_rows[0] = load_rows(oldmap, 0, 0, T2, "old_rows")
+                w5_rows = [[load_rows(w5, a, j * CHUNK) for a in range(2)] for j in range(N // CHUNK)]
+                for j in range(T2 // CHUNK):
+                    weave_old(0, j)
+                old_rows[1] = load_rows(oldmap, 1, 0, T2, "old_rows")
+            if c in (SLICES_PER_PASS - 1, SLICES_PER_PASS):
+                w5_stages.append(staged(w5_rows[len(w5_stages)], "raw"))
+            if c >= SLICES_PER_PASS:
+                weave_old(1, c - SLICES_PER_PASS)
+
+        m0, free_banks = 0, list(SCORE_BANKS)
         for width in OUT_WIDTHS:
-            banks = N // P * width // BANK
-            strengthened(1, m0, width)
-            scores(m0, width, [SCORE_BANKS[used + i] for i in range(banks)])
-            m0, used = m0 + width, used + banks
+            count = N // P * width // BANK
+            strengthen(1, m0, width)
+            score(m0, width, free_banks[:count])
+            m0, free_banks = m0 + width, free_banks[count:]

from contextlib import ExitStack

import concourse.mybir as mybir
from concourse.masks import make_identity

K, K2, T, S, H, T2, N = 1024, 512, 2048, 512, 1024, 1024, 512
FLOPS = 2 * S * H * (2 * K + 2 * K2) + 2 * H * N * T2

F32 = mybir.dt.float32
BF16 = mybir.dt.bfloat16
I32 = mybir.dt.int32
U32 = mybir.dt.uint32
U16 = mybir.dt.uint16
U8 = mybir.dt.uint8
FP8X4 = mybir.dt.float8_e4m3fn_x4
FP4X4 = mybir.dt.float4_e2m1fn_x4
ALU = mybir.AluOpType
ACT = mybir.ActivationFunctionType

P = 128
PACK = 4
K_PASS = P * PACK
QUADRANT = 32
BANK = 512
CHUNK = 256
SLICES = H // P
LAST = SLICES - 1
SLICES_PER_PASS = K_PASS // P

B_BEFORE = 4
PAGES_B = 4
AHEAD = 3
W3_WIDTHS = (128, 128, 256, 256, 256)
W4_HEAD = 256
OUT_WIDTHS = (256, 256, 256, 128, 128)
RING_BUFS = {"raw": 10, "woven": 6, "copied": 3, "feature": 3, "magnitude": 3, "z": 3, "old_rows": 1, "w1_early_end": 1}
PSUM_BUFS = {"first": 1, "second": 3, "sum": 2, "back": 2}
SCORE_BANKS = ("second", "second", "second", "first", "second", "second", "sum", "sum")


def tile_list_street_change_scores_kernel(
    tc, tab_words, tab_scales, tab2_words, tab2_scales, offs, offs2, offs3, offs4,
    w1, w2_words, w2_scales, w3, w4_words, w4_scales, wg1, wg2, oldmap, w5, out,
):
    nc = tc.nc
    with ExitStack() as ctx:
        keep = ctx.enter_context(tc.tile_pool(name="keep", bufs=1))
        ring = ctx.enter_context(tc.tile_pool(name="ring", bufs=1))
        psum = ctx.enter_context(tc.psum_pool(name="psum", bufs=1))

        def sbuf(name, shape, dtype, slot=None):
            slot = slot or name
            if slot in RING_BUFS:
                return ring.tile(shape, dtype, name=name, tag=slot, bufs=RING_BUFS[slot], align_bytes=64)
            return keep.tile(shape, dtype, name=name, tag=slot, align_bytes=64)

        def bank(tag, shape=(P, BANK)):
            return psum.tile(list(shape), F32, name=tag, tag=tag, bufs=PSUM_BUFS[tag])

        def load(name, source, dtype):
            tile = sbuf(name, list(source.shape), dtype)
            nc.sync.dma_start(tile[:], source)
            return tile

        def load_words(name, source, dtype):
            tile = sbuf(name, [P, source.shape[1] // (1 if dtype == U8 else PACK)], dtype)
            nc.sync.dma_start(tile[:].bitcast(I32), source.bitcast(I32))
            return tile

        def cleared_plane(name, width):
            plane = sbuf(name, [P, width], U8)
            nc.gpsimd.memset(plane[:].bitcast(I32), 0)
            return plane

        def load_plane(plane, source):
            for q in range(P // QUADRANT):
                nc.sync.dma_start(
                    plane[QUADRANT * q : QUADRANT * q + 4, :].bitcast(I32).rearrange("r (a t) -> r a t", a=source.shape[0]),
                    source[:, 4 * q : 4 * q + 4, :].bitcast(I32).rearrange("a r t -> r a t"),
                )

        def load_rows(source, a, c0, width=CHUNK, slot="raw"):
            rows = sbuf("rows", [P, PACK, width], F32, slot)
            block = source[a * K_PASS : (a + 1) * K_PASS, c0 : c0 + width]
            nc.sync.dma_start(rows[:], block.rearrange("(p t) c -> p t c", t=PACK))
            return rows

        def weave(dst, src):
            nc.scalar.copy(dst.rearrange("p (c i t) -> p c t i", i=4, t=PACK), src.rearrange("p t (c i) -> p c t i", i=4))

        def staged(passes, slot="woven"):
            size = PACK * passes[0].shape[2]
            stage = sbuf("stage", [P, len(passes) * size], BF16, slot)
            for a, rows in enumerate(passes):
                weave(stage[:, a * size : (a + 1) * size], rows[:])
            return stage

        def quantised(name, values):
            width = values.shape[1] // PACK
            codes = sbuf(name + "_codes", [P, width], U32)
            plane = sbuf(name + "_plane", [P, width], U8)
            nc.vector.quantize_mx(out=codes[:].bitcast(FP8X4), scales=plane[:], in_=values)
            return codes, plane

        def gathered(name, window, offsets, dtype):
            tile = sbuf(name, [P, S], dtype)
            nc.vector.tensor_copy(tile[:], window[:].indirect(offsets[:]))
            return tile

        def mx(result, lhs, lhs_plane, rhs, rhs_plane, start, stop):
            nc.tensor.matmul_mx(out=result, lhsT=lhs, lhsT_scale=lhs_plane, rhs=rhs.bitcast(FP8X4),
                                rhs_scale=rhs_plane, start=start, stop=stop)

        pages = {}

        def clear_page(kind, i, slot):
            pages[kind, i] = sbuf("page_%s%d" % (kind, i), [P, T2], F32, slot)
            nc.gpsimd.memset(pages[kind, i][:], 0.0)

        def page_of(kind, c):
            if kind == "b":
                return pages[kind, c % PAGES_B]
            return pages[kind, min(c, LAST - 1) % 2]

        steps = [("b", c) for c in range(B_BEFORE + 1)] + [("a", c) for c in range(B_BEFORE)]
        for c in range(B_BEFORE, SLICES):
            steps.extend([("b", c + 1), ("a", c)] if c < LAST else [("a", c)])

        feature_slot = {("b", 0): "page_b2", ("b", 1): "w3_third", ("b", 2): "w3_third", ("b", 3): "b2_copied",
                        ("b", B_BEFORE): "tab_sb1",
                        ("a", 4): "tab_sb1", ("a", 5): "tab2_sb", ("a", 6): "w3_third", ("a", 7): "tab_sb1"}
        copied_slot = {("b", 1): "ident", ("b", 2): "b2_copied", ("b", 3): "page_a0", ("b", B_BEFORE): "w1_early_end"}
        first_pass_done = steps.index(("a", SLICES_PER_PASS))

        tab2_plane = cleared_plane("tab2_plane", tab2_scales.shape[2])
        w4_plane = cleared_plane("w4_plane", H)
        tab_plane = cleared_plane("tab_plane", T)
        v_plane1 = cleared_plane("v_plane1", S)
        w2_plane = cleared_plane("w2_plane", 2 * H)

        as_bytes = "p c i -> p (c i)"
        w3_starts = [sum(W3_WIDTHS[:j]) for j in range(len(W3_WIDTHS))]
        w4_bytes = w4_words[0].rearrange(as_bytes)
        list2 = load("list2", offs2, U16)
        load_plane(tab2_plane, tab2_scales)
        tab2_sb = load_words("tab2_sb", tab2_words[0].rearrange(as_bytes), U32)
        w3_rows = [load_rows(w3, 0, 0, W3_WIDTHS[0])]
        w4_head = load_words("w4_head", w4_bytes[:, : PACK * W4_HEAD], U32)
        load_plane(w4_plane, w4_scales)
        w3_rows.append(load_rows(w3, 0, w3_starts[1], W3_WIDTHS[1]))
        list4 = load("list4", offs4, U16)
        wg2_sb = load("wg2_sb", wg2, F32)
        w3_rows.append(load_rows(w3, 0, w3_starts[2]))
        w4_rest = load_words("w4_rest", w4_bytes[:, PACK * W4_HEAD :], U32)
        list1 = load("list1", offs, U16)
        for q in range(P // QUADRANT):
            nc.sync.dma_start(tab_plane[QUADRANT * q : QUADRANT * q + 8, :].bitcast(I32),
                              tab_scales[:, 4 * q : 4 * q + 4, :].bitcast(I32))
        w3_rows.append(load_rows(w3, 0, w3_starts[3]))
        w1_early = [[load_rows(w1, a, 0) for a in range(2)],
                    [load_rows(w1, 0, CHUNK), load_rows(w1, 1, CHUNK, slot="w1_early_end")]]
        v2_plane = gathered("v2_plane", tab2_plane, list2, U8)
        v2_words = gathered("v2_words", tab2_sb, list2, U32)

        w3_mx, w1_mx, w5_mx, z_mx = {}, {}, {}, {}
        v_words, w5_stages, ident = [], [], []
        products, features, sums, magnitudes, old_rows, old_woven = {}, {}, {}, {}, {}, {}

        def multiply(step):
            kind, c = step
            i = steps.index(step)
            first = bank("back" if i <= first_pass_done and i % 3 else "first")
            second = bank("second")
            if kind == "b":
                j = max(n for n, start in enumerate(w3_starts) if start <= c * P)
                local = slice(c * P - w3_starts[j], (c + 1) * P - w3_starts[j])
                w4_cols = w4_head[:, c * P : (c + 1) * P] if c * P < W4_HEAD else w4_rest[:, c * P - W4_HEAD : (c + 1) * P - W4_HEAD]
                weights = [(w4_cols, w4_plane[:, c * P : (c + 1) * P]), (w3_mx[j][0][:, local], w3_mx[j][1][:, local])]
                for result, (codes, plane) in zip((first, second), weights if c else weights[::-1]):
                    mx(result[:], codes.bitcast(FP8X4), plane, v2_words[:], v2_plane[:], True, True)
            else:
                for a in range(2):
                    mx(first[:], w2_sb[a][:, 2 * c * P : 2 * (c + 1) * P].bitcast(FP4X4),
                       w2_plane[:, a * H + c * P : a * H + (c + 1) * P], v_words[a][:],
                       (v_plane, v_plane1)[a][:], a == 0, a == 1)
                codes, plane = w1_mx[c * P // CHUNK]
                for a in range(2):
                    local = slice(a * CHUNK + c * P % CHUNK, a * CHUNK + c * P % CHUNK + P)
                    mx(second[:], codes[:, local].bitcast(FP8X4), plane[:, local], v_words[a][:], v_plane[4 * a :, :],
                       a == 0, a == 1)
            copied = sbuf("copy_of_first", [P, S], F32, copied_slot.get(step, "copied"))
            nc.scalar.copy(copied[:], first[:])
            products[step] = (copied, second)

        def join(step):
            copied, second = products[step]
            features[step] = sbuf("feature_of_step", [P, S], F32, feature_slot.get(step, "feature"))
            nc.vector.tensor_tensor(features[step][:], second[:], copied[:], ALU.mult if step[0] == "b" else ALU.max)
            if step == ("b", 1):
                ident.append(sbuf("ident", [P, P], F32))
                make_identity(nc, ident[0][:])
            if step == ("b", 3):
                clear_page("a", 0, copied_slot[step])
            if step == ("b", B_BEFORE):
                clear_page("a", 1, copied_slot[step])

        def place(step):
            offsets, weight = (list4, wg2_sb) if step[0] == "b" else (list3, wg1_sb)
            nc.vector.tensor_tensor(page_of(*step)[:].indirect(offsets[:]), features[step][:], weight[:], ALU.mult)

        def turn(result, page, half, start, stop):
            for i in range(4):
                m0 = (4 * half + i) * P
                nc.tensor.matmul(result[:, i * P : (i + 1) * P], page[:, m0 : m0 + P], ident[0][:],
                                 start=start and i == 0, stop=stop and i == 3, is_transpose=True)

        def open_sum(c):
            sums[c] = [bank(tag) for tag in (("first", "second") if c == LAST else ("sum", "sum"))]
            for half in range(2):
                turn(sums[c][half], page_of("b", c), half, True, False)

        def close_sum(c):
            b, quarter = divmod(c, SLICES_PER_PASS)
            for half in range(2):
                if quarter == 0:
                    slot = "tab_sb0" if (b, half) == (1, 1) else "magnitude"
                    magnitudes[b, half] = sbuf("magnitude_of_half", [P, 4, PACK, P], F32, slot)
                turn(sums[c][half], page_of("a", c), half, False, True)
                nc.scalar.activation(magnitudes[b, half][:, :, :, QUADRANT * quarter : QUADRANT * (quarter + 1)],
                                     sums[c][half][:].rearrange("m (i q t) -> m i t q", i=4, t=PACK), ACT.Abs)

        def weave_old(b, j):
            old_woven[b, j] = sbuf("old_woven", [P, PACK * CHUNK], F32, ("woven", "raw")[b])
            weave(old_woven[b, j][:], old_rows[b][:, :, j * CHUNK : (j + 1) * CHUNK])

        def strengthen(b, m0, width, slot="z"):
            z = sbuf("z_values", [P, PACK * CHUNK], BF16, slot)
            for i in range(width // P):
                block = m0 // P + i
                back = bank("sum" if b == 1 and block % 4 < 2 else "back", (P, PACK, P))
                for t in range(PACK):
                    nc.tensor.transpose(back[:, t, :], magnitudes[b, block // 4][:, block % 4, t, :], ident[0][:])
                old = old_woven[b, block // 2][:, (block % 2) * BANK : (block % 2 + 1) * BANK]
                nc.vector.scalar_tensor_tensor(
                    z[:, i * BANK : (i + 1) * BANK].rearrange("p (m t) -> p m t", t=PACK),
                    back[:].rearrange("p t m -> p m t"), 1.0, old.rearrange("p (m t) -> p m t", t=PACK), ALU.add, ALU.mult)
            codes, plane = quantised("z%d_%d" % (b, m0), z[:, : PACK * width])
            for i in range(width // P):
                z_mx[b, m0 + i * P] = (codes[:, i * P :], plane[:, i * P :])

        def score(m0, width, tags):
            per_bank = BANK // width
            for n0, tag in zip(range(0, N // P, per_bank), tags):
                sums_n = bank(tag)
                for b in range(2):
                    z_codes, z_plane = z_mx[b, m0]
                    for i in range(per_bank):
                        codes, plane = w5_mx[(n0 + i) * P // CHUNK]
                        c0 = b * CHUNK + (n0 + i) * P % CHUNK
                        mx(sums_n[:, i * width : (i + 1) * width], codes[:, c0 : c0 + P].bitcast(FP8X4), plane[:, c0 : c0 + P],
                           z_codes[:, :width], z_plane[:, :width], b == 0 and i == 0, b == 1 and i == per_bank - 1)
                result = sbuf("result", [P, per_bank, width], F32, "raw")
                nc.scalar.activation(result[:], sums_n[:].rearrange("p (n m) -> p n m", m=width), ACT.Tanh)
                nc.sync.dma_start(out.rearrange("(n p) m -> p n m", p=P)[:, n0 : n0 + per_bank, m0 : m0 + width], result[:])

        w3_mx[0] = quantised("w3_0", staged([w3_rows[0]], "page_b0")[:])
        clear_page("b", 0, "page_b0")
        multiply(steps[0])
        join(steps[0])
        w3_mx[1] = quantised("w3_1", staged([w3_rows[1]], "page_b1")[:])
        clear_page("b", 1, "page_b1")
        load_plane(w2_plane, w2_scales)
        w2_sb = [load_words("w2_sb%d" % a, w2_words[a], U8) for a in range(2)]
        list3 = load("list3", offs3, U16)
        wg1_sb = load("wg1_sb", wg1, F32)
        tab_sb = [load_words("tab_sb%d" % a, tab_words[a].rearrange(as_bytes), U32) for a in range(2)]
        multiply(steps[1])
        w3_mx[2] = quantised("w3_2", staged([w3_rows[2]], "w3_third")[:])
        multiply(steps[2])
        v_plane = gathered("v_plane", tab_plane, list1, U8)
        clear_page("b", 3, "tab_plane")
        for q in range(P // QUADRANT):
            nc.sync.dma_start(v_plane1[QUADRANT * q : QUADRANT * q + 4, :].bitcast(I32),
                              v_plane[QUADRANT * q + 4 : QUADRANT * q + 8, :].bitcast(I32))

        for i, step in enumerate(steps):
            kind, c = step
            following = steps[i + 1 : i + 2]
            same_slot = [s for s in following if step in feature_slot and feature_slot.get(s) == feature_slot[step]]
            for s in following:
                if s not in same_slot:
                    join(s)
            place(step)
            for s in same_slot:
                join(s)
            if step == ("b", 0):
                clear_page("b", 2, feature_slot[step])
            if step == ("b", 1):
                w3_mx[3] = quantised("w3_3", staged([w3_rows[3]])[:])
                for j, passes in enumerate(w1_early):
                    w1_mx[j] = quantised("w1_%d" % j, staged(passes)[:])
                v_words.extend(gathered("v_words%d" % a, tab_sb[a], list1, U32) for a in range(2))
            if step == ("b", B_BEFORE):
                w1_mx[2] = quantised("w1_2", staged([load_rows(w1, a, 2 * CHUNK) for a in range(2)])[:])
                w3_mx[4] = quantised("w3_4", staged([load_rows(w3, 0, w3_starts[4])])[:])
                w1_mx[3] = quantised("w1_3", staged([load_rows(w1, a, 3 * CHUNK) for a in range(2)])[:])
            if i + AHEAD < len(steps):
                multiply(steps[i + AHEAD])
            if step == ("a", LAST):
                w5_codes = sbuf("w5_codes", [P, 2 * N], U32, "wg1_sb")
                w5_plane = sbuf("w5_plane", [P, 2 * N], U8)
                for j, stage in enumerate(w5_stages):
                    cols = slice(j * N, (j + 1) * N)
                    nc.vector.quantize_mx(out=w5_codes[:, cols].bitcast(FP8X4), scales=w5_plane[:, cols], in_=stage[:])
                    w5_mx[j] = (w5_codes[:, cols], w5_plane[:, cols])
            if kind == "a" and c >= SLICES_PER_PASS:
                strengthen(0, (c - SLICES_PER_PASS) * CHUNK, CHUNK, feature_slot[step])
            if step in (("b", 0), ("b", LAST)):
                open_sum(c)
            if kind == "b":
                continue
            close_sum(c)
            if c + 1 < LAST:
                open_sum(c + 1)
            if c == 0:
                old_rows[0] = load_rows(oldmap, 0, 0, T2, "old_rows")
                w5_rows = [[load_rows(w5, a, j * CHUNK) for a in range(2)] for j in range(N // CHUNK)]
                for j in range(T2 // CHUNK):
                    weave_old(0, j)
                old_rows[1] = load_rows(oldmap, 1, 0, T2, "old_rows")
            if c in (SLICES_PER_PASS - 1, SLICES_PER_PASS):
                w5_stages.append(staged(w5_rows[len(w5_stages)], "raw"))
            if c >= SLICES_PER_PASS:
                weave_old(1, c - SLICES_PER_PASS)

        m0, free_banks = 0, list(SCORE_BANKS)
        for width in OUT_WIDTHS:
            count = N // P * width // BANK
            strengthen(1, m0, width)
            score(m0, width, free_banks[:count])
            m0, free_banks = m0 + width, free_banks[count:]
